import numpy as np
import ml_dtypes


def mxq(x, axis, fmt="e4m3"):
    dtype, down = {"e4m3": (ml_dtypes.float8_e4m3fn, 7), "e5m2": (ml_dtypes.float8_e5m2, 14)}[fmt]
    v = np.moveaxis(np.asarray(x, np.float32).astype(ml_dtypes.bfloat16).astype(np.float64), axis, -1)
    blocks = v.reshape(v.shape[:-1] + (-1, 32))
    amax = np.abs(blocks).max(-1, keepdims=True)
    byte = np.maximum(np.where(amax > 0, np.frexp(amax)[1] - 1 + 127, 0) - down, 1)
    scale = np.exp2(byte - 127.0)
    codes = (blocks / scale).astype(np.float32).astype(dtype).astype(np.float64)
    return np.moveaxis((codes * scale).reshape(v.shape), -1, axis)


WIDE = False


def mx_kscale(k):
    if not WIDE:
        return np.ones(k)
    levels = np.array([10, -10, 5, -5, 0])
    if k % 512:
        return np.exp2(np.random.permutation(np.resize(levels, k // 32))).repeat(32)
    a = np.empty((k // 512, 16))
    for p in range(k // 512):
        a[p, :8] = np.random.permutation(np.resize(levels, 8))
        for g in range(8):
            far = levels[np.abs(levels - a[p, g]) >= 10]
            a[p, g + 8] = far[np.random.randint(len(far))]
    return np.exp2(a.ravel()).repeat(32)


BF16 = ml_dtypes.bfloat16


def bf(x):
    return np.asarray(x, np.float32).astype(BF16)


def f64(x):
    return np.asarray(x).astype(np.float64)


E2M1 = np.array([0.0, 0.5, 1.0, 1.5, 2.0, 3.0, 4.0, 6.0, -0.0, -0.5, -1.0, -1.5, -2.0, -3.0, -4.0, -6.0])


def pack_weight(w, fmt):
    k, n = w.shape
    w = f64(bf(w)).reshape(k // 32, 32, n)
    amax = np.abs(w).max(1)
    if fmt == "e4m3":
        byte = np.frexp(amax)[1] - 1 + 127 - 7
    else:
        mant, ex = np.frexp(amax / 6.0)
        byte = np.where(mant > 0.5, ex, ex - 1) + 127
    byte = np.clip(np.where(amax > 0, byte, 1), 1, 254)
    scaled = (w * np.exp2(127.0 - byte)[:, None, :]).reshape(k, n).astype(np.float32)
    by_word = np.ascontiguousarray(scaled.reshape(k // 512, 128, 4, n).transpose(0, 1, 3, 2))
    if fmt == "e4m3":
        words = by_word.astype(ml_dtypes.float8_e4m3fn).view(np.uint8)
    else:
        c = by_word.astype(ml_dtypes.float4_e2m1fn).view(np.uint8) & 0xF
        words = c[..., 0::2] | (c[..., 1::2] << 4)
    return np.ascontiguousarray(words), np.ascontiguousarray(byte.astype(np.uint8).reshape(k // 512, 16, n))


def unpack_weight(words, scales, fmt):
    g, p, n, _ = words.shape
    if fmt == "e4m3":
        vals = np.ascontiguousarray(words).view(ml_dtypes.float8_e4m3fn).astype(np.float64)
    else:
        nib = np.empty((g, p, n, 4), np.uint8)
        nib[..., 0::2] = words & 0xF
        nib[..., 1::2] = words >> 4
        vals = E2M1[nib]
    vals = vals * np.repeat(np.exp2(scales.astype(np.float64) - 127.0), 8, axis=1)[..., None]
    return vals.transpose(0, 1, 3, 2).reshape(g * 512, n)
def pack4(w):
    words, scales = pack_weight(w, "e2m1")
    return words.reshape(words.shape[0], 128, -1), scales


def unpack4(words, scales):
    return unpack_weight(words.reshape(words.shape[0], 128, -1, 2), scales, "e2m1")


def planes(Y):
    n, m = Y.shape
    b = f64(bf(Y)).reshape(n // 32, 32, m)
    amax = np.abs(b).max(1)
    byte = np.clip(np.where(amax > 0, np.frexp(amax)[1] - 1 + 127 - 7, 1), 1, 254)
    codes = (b * np.exp2(127.0 - byte)[:, None, :]).reshape(n, m).astype(np.float32).astype(ml_dtypes.float8_e4m3fn).view(np.uint8)
    words = codes.reshape(n // 512, 128, 4, m).transpose(0, 1, 3, 2)
    return np.ascontiguousarray(words), np.ascontiguousarray(byte.astype(np.uint8).reshape(n // 512, 16, m))


T, C, TAPS, DELAY, D = 1024, 512, 3, 3, 1536


def setup_inputs():
    s = mx_kscale(T)
    t = mx_kscale(D)
    loud = np.exp(0.25 * np.random.randn(T + DELAY + TAPS - 1, 1))
    z = loud * np.random.randn(T + DELAY + TAPS - 1, C)
    x = np.concatenate([z[TAPS - 1 - j:TAPS - 1 - j + T] for j in range(TAPS)], axis=1)
    lam = np.mean(z[TAPS - 1 + DELAY:TAPS - 1 + DELAY + T] ** 2, axis=1, keepdims=True)
    v = x / lam / np.sqrt(T)
    v_words, v_scales = pack4(v * s[:, None])
    x_words, x_scales = pack4(x * t[None, :] / s[:, None])
    a = np.random.randn(D, D)
    loading = bf((0.3 * (a + a.T) + np.sqrt(T) * np.eye(D)) * t[None, :])
    filt = bf(np.random.randn(D, C) / np.sqrt(D) / t[:, None])
    step = 0.4 * np.exp(0.8 * np.random.randn(D))
    return {"v_words": v_words, "v_scales": v_scales,
            "x_words": x_words, "x_scales": x_scales,
            "loading": loading, "filt": filt,
            "rhs": bf(np.random.randn(D, C)),
            "step": bf(step),
            "beta": bf(0.5 * np.exp(0.2 * np.random.randn(C))),
            "p_old": bf(2.0 * step[:, None] * np.random.randn(D, C))}


def reference(v_words, v_scales, x_words, x_scales, loading, filt, rhs, step, beta, p_old):
    V = unpack4(v_words, v_scales)
    X = unpack4(x_words, x_scales)
    R = (V.T @ X) + f64(loading)
    RF = mxq(R, 1, "e4m3") @ mxq(f64(filt), 0, "e4m3")
    y = f64(step)[:, None] * (f64(rhs) - RF) + f64(beta)[None, :] * f64(p_old)
    Y = y.reshape(D, C)
    words, scales = planes(Y)
    return y, words, scales

@@ -1,0 +1,516 @@
+from contextlib import ExitStack
+
+import concourse.mybir as mybir
+from concourse.masks import make_identity
+
+F32 = mybir.dt.float32
+BF16 = mybir.dt.bfloat16
+I32 = mybir.dt.int32
+U32 = mybir.dt.uint32
+U8 = mybir.dt.uint8
+FP4X4 = mybir.dt.float4_e2m1fn_x4
+FP8X4 = mybir.dt.float8_e4m3fn_x4
+ALU = mybir.AluOpType
+
+T, D, C = 1024, 1536, 512
+FLOPS = 2 * T * D * D + 2 * D * D * C
+
+P = 128
+G = 512
+NG = D // G
+NT = T // G
+NB = NG * NG
+
+ORDER = [
+    ("head",),
+    ("lf", 0),
+    ("lb", 0, 0, 2),
+    ("mm", 0, 0),
+    ("lsmall",),
+    ("add", 0, 0),
+    ("mm", 0, 1),
+    ("lb", 0, 2, 4),
+    ("mm", 0, 2),
+    ("add", 0, 1),
+    ("F", 0),
+    ("lx", 1),
+    ("mm", 0, 3),
+    ("mm", 1, 0),
+    ("add", 0, 2),
+    ("lb", 1),
+    ("mm", 1, 1),
+    ("T", 0, 0, 2, 4),
+    ("lx", 2),
+    ("add", 0, 3),
+    ("lo", 0),
+    ("lb", 2),
+    ("lvs",),
+    ("add", 1, 0),
+    ("beta",),
+    ("C", 0, 0, 2),
+    ("T", 0, 2, 4, 5),
+    ("add", 1, 1),
+    ("lr", 0),
+    ("mm", 1, 2),
+    ("Qf", 0),
+    ("mm", 1, 3),
+    ("lv", 1),
+    ("mm", 2, 0),
+    ("add", 1, 2),
+    ("lf", 1),
+    ("add", 1, 3),
+    ("mm", 2, 1),
+    ("C", 0, 2, 4),
+    ("add", 2, 0),
+    ("T", 1, 0, 2, 4),
+    ("T", 1, 2, 4, 5),
+    ("B1", 0),
+    ("C", 1, 0, 2),
+    ("C", 1, 2, 4),
+    ("add", 2, 1),
+    ("lb", 3),
+    ("mm", 2, 2),
+    ("Q", 0),
+    ("lf", 2),
+    ("B2", 0, 0),
+    ("Q", 1),
+    ("add", 2, 2),
+    ("mm", 2, 3),
+    ("mm", 3, 0),
+    ("T", 2, 0, 2, 4),
+    ("mm", 3, 1),
+    ("mm", 3, 2),
+    ("B2", 0, 1),
+    ("S", 0, 0, 0, 6),
+    ("add", 2, 3),
+    ("F", 1),
+    ("add", 3, 0),
+    ("add", 3, 1),
+    ("lb", 4),
+    ("mm", 3, 3),
+    ("lv", 2),
+    ("B1", 1),
+    ("lb", 5),
+    ("lo", 1),
+    ("C", 2, 0, 2),
+    ("mm", 4, 0),
+    ("mm", 4, 1),
+    ("F", 2),
+    ("T", 2, 2, 4, 5),
+    ("add", 3, 2),
+    ("mm", 4, 2),
+    ("S", 0, 1, 0, 7),
+    ("add", 3, 3),
+    ("mm", 4, 3),
+    ("Qf", 1),
+    ("B2", 0, 2),
+    ("add", 4, 0),
+    ("add", 4, 1),
+    ("T", 3, 0, 2, 4),
+    ("C", 2, 2, 4),
+    ("T", 3, 2, 4, 5),
+    ("Qf", 2),
+    ("mm", 5, 0),
+    ("lr", 2),
+    ("add", 4, 2),
+    ("B2", 0, 3),
+    ("Q", 2),
+    ("B1", 2),
+    ("S", 0, 1, 1, 7),
+    ("mm", 5, 1),
+    ("mm", 5, 2),
+    ("lr", 1),
+    ("C", 3, 0, 2),
+    ("C", 3, 2, 4),
+    ("add", 4, 3),
+    ("S", 0, 1, 2, 7),
+    ("S", 0, 0, 1, 6),
+    ("add", 5, 0),
+    ("add", 5, 1),
+    ("mm", 5, 3),
+    ("S", 0, 0, 2, 6),
+    ("add", 5, 2),
+    ("add", 5, 3),
+    ("Y", 0, 0),
+    ("Q", 3),
+    ("B2", 1, 0),
+    ("lb", 6),
+    ("T", 4, 0, 2, 4),
+    ("T", 4, 2, 4, 5),
+    ("B2", 1, 1),
+    ("C", 4, 0, 2),
+    ("C", 4, 2, 4),
+    ("mm", 6, 0),
+    ("mm", 6, 1),
+    ("T", 5, 0, 2, 4),
+    ("T", 5, 2, 4, 5),
+    ("Y", 0, 1),
+    ("add", 6, 0),
+    ("S", 0, 2, 0, 6),
+    ("mm", 6, 2),
+    ("S", 0, 2, 1, 6),
+    ("lb", 7),
+    ("add", 6, 1),
+    ("B1", 3),
+    ("lo", 2),
+    ("C", 5, 0, 2),
+    ("mm", 6, 3),
+    ("mm", 7, 0),
+    ("S", 0, 2, 2, 6),
+    ("add", 6, 2),
+    ("add", 6, 3),
+    ("S", 0, 3, 0, 7),
+    ("lb", 8),
+    ("C", 5, 2, 4),
+    ("add", 7, 0),
+    ("S", 0, 3, 1, 7),
+    ("B2", 1, 2),
+    ("B2", 1, 3),
+    ("mm", 7, 1),
+    ("S", 0, 3, 2, 7),
+    ("Q", 4),
+    ("Y", 0, 2),
+    ("T", 6, 0, 2, 4),
+    ("T", 6, 2, 4, 5),
+    ("add", 7, 1),
+    ("Y", 0, 3),
+    ("mm", 7, 2),
+    ("add", 7, 2),
+    ("mm", 7, 3),
+    ("mm", 8, 0),
+    ("add", 7, 3),
+    ("C", 6, 0, 2),
+    ("S", 1, 0, 0, 6),
+    ("S", 1, 1, 0, 7),
+    ("Q", 5),
+    ("mm", 8, 1),
+    ("C", 6, 2, 4),
+    ("B1", 4),
+    ("mm", 8, 2),
+    ("S", 1, 0, 1, 6),
+    ("S", 1, 0, 2, 6),
+    ("S", 1, 1, 1, 7),
+    ("add", 8, 0),
+    ("B2", 2, 0),
+    ("S", 1, 1, 2, 7),
+    ("I", 0, 0),
+    ("Q", 6),
+    ("Y", 1, 0),
+    ("T", 7, 0, 2, 4),
+    ("B2", 2, 1),
+    ("Y", 1, 1),
+    ("st", 1, 0, 2),
+    ("T", 7, 2, 4, 5),
+    ("mm", 8, 3),
+    ("add", 8, 1),
+    ("S", 1, 2, 0, 6),
+    ("C", 7, 0, 2),
+    ("C", 7, 2, 4),
+    ("S", 1, 2, 1, 6),
+    ("add", 8, 2),
+    ("add", 8, 3),
+    ("S", 1, 2, 2, 6),
+    ("S", 1, 3, 0, 7),
+    ("S", 1, 3, 1, 7),
+    ("S", 1, 3, 2, 7),
+    ("T", 8, 0, 2, 4),
+    ("T", 8, 2, 3, 5),
+    ("B1", 5),
+    ("Y", 1, 2),
+    ("T", 8, 3, 4, 6),
+    ("S", 2, 0, 0, 0),
+    ("C", 8, 0, 2),
+    ("S", 2, 3, 0, 3),
+    ("C", 8, 2, 3),
+    ("st", 0, 0, 2),
+    ("C", 8, 3, 4),
+    ("Y", 1, 3),
+    ("Qy", 0),
+    ("Q", 7),
+    ("I", 1, 0),
+    ("Q", 8, 0, 2),
+    ("B2", 2, 2),
+    ("S", 2, 1, 0, 1),
+    ("S", 2, 2, 0, 2),
+    ("S", 2, 1, 1, 1),
+    ("S", 2, 0, 1, 0),
+    ("S", 2, 3, 1, 3),
+    ("S", 2, 0, 2, 0),
+    ("st", 0, 2, 4),
+    ("Q", 8, 2, 4),
+    ("B2", 2, 3),
+    ("S", 2, 1, 2, 1),
+    ("S", 2, 3, 2, 3),
+    ("st", 1, 2, 4),
+    ("Y", 2, 0, 0, 256),
+    ("S", 2, 2, 1, 2),
+    ("S", 2, 2, 2, 2),
+    ("Y", 2, 1, 0, 256),
+    ("Qy", 1),
+    ("Y", 2, 2, 0, 256),
+    ("Y", 2, 3, 0, 256),
+    ("Y", 2, 0, 256, 512),
+    ("Y", 2, 1, 256, 512),
+    ("I", 2, 0, 0, 256),
+    ("st", 2, 0, 4, 0, 256),
+    ("Y", 2, 2, 256, 512),
+    ("Y", 2, 3, 256, 512),
+    ("I", 2, 1, 256, 512),
+    ("st", 2, 0, 4, 256, 512),
+    ("Qy", 2, 0, 256),
+    ("Qy", 2, 256, 512),
+    ("ss",),
+]
+
+
+def tile_wpe_search_direction_k5_kernel(
+    tc, v_words, v_scales, x_words, x_scales, loading, filt, rhs, step, beta, p_old, out_0, out_1, out_2
+):
+    nc = tc.nc
+    with ExitStack() as ctx:
+        keep = ctx.enter_context(tc.tile_pool(name="keep", bufs=1))
+        stage = ctx.enter_context(tc.tile_pool(name="stage", bufs=1))
+        psum = ctx.enter_context(tc.psum_pool(name="psum", bufs=1))
+        ctx.enter_context(tc.manual_schedule())
+
+        def kept(name, shape, dtype):
+            return keep.tile(shape, dtype, name=name, align_bytes=64)
+
+        v_sb = [kept("v_sb%d" % g, [P, NT, 2 * G], U8) for g in range(NG)]
+        x_sb = [kept("x_sb%d" % g, [P, NT, 2 * G], U8) for g in range(NG)]
+        v_sc_first = kept("v_sc_first", [P, NT, G], U8)
+        v_sc_rest = kept("v_sc_rest", [P, NT, D - G], U8)
+        x_sc = kept("x_sc", [P, NT, D], U8)
+        load_sb = [kept("load_sb%d" % g, [P, 4, D], BF16) for g in range(NG)]
+        filt_sb = [kept("filt_sb%d" % g, [P, 4, C], BF16) for g in range(NG)]
+        rhs_sb = [kept("rhs_sb%d" % g, [P, 4, C], BF16) for g in range(NG)]
+        old_sb = [kept("old_sb%d" % g, [P, 4, C], BF16) for g in range(NG)]
+        y_sb = [kept("y_sb%d" % g, [P, 4, C], F32) for g in range(NG)]
+        r_codes = [kept("r_codes%d" % b, [P, G], U32) for b in range(NB)]
+        r_scales = [kept("r_scales%d" % b, [P, G], U8) for b in range(NB)]
+        f_codes = [kept("f_codes%d" % g, [P, C], U32) for g in range(NG)]
+        f_scales = [kept("f_scales%d" % g, [P, C], U8) for g in range(NG)]
+        y_codes = [kept("y_codes%d" % g, [P, C], U32) for g in range(NG)]
+        y_scales = kept("y_scales", [P, NG, C], U8)
+        ident = kept("ident", [P, P], F32)
+        step_bf = kept("step_bf", [P, NG, 4], BF16)
+        step_pos = kept("step_pos", [P, NG * 4], F32)
+        step_neg = kept("step_neg", [P, NG * 4], F32)
+        beta_bf = kept("beta_bf", [P, 4], BF16)
+        beta_col = kept("beta_col", [P, 4], F32)
+        beta_all = kept("beta_all", [P, C], BF16)
+
+        def bank(n, shape):
+            return psum.tile(shape, F32, name="bank%d" % n, tag="bank%d" % n)
+
+        def load_words(dst, src, g):
+            view = src.bitcast(I32).rearrange("k p w -> p k w")
+            nc.sync.dma_start(out=dst[:].bitcast(I32), in_=view[:, :, g * 256:(g + 1) * 256])
+
+        def load_scales(queue, dst, src, c0, c1, quadrants):
+            view = src.bitcast(I32)
+            for q in quadrants:
+                rows = view[:, 4 * q:4 * q + 4, c0 // 4:c1 // 4].rearrange("k r w -> r k w")
+                queue.dma_start(out=dst[32 * q:32 * q + 4, :, :].bitcast(I32), in_=rows)
+
+        def load_loading(g, u0, u1, c0, c1):
+            rows = loading[g * G:(g + 1) * G, :].rearrange("(u p) j -> p u j", p=P)
+            nc.sync.dma_start(out=load_sb[g][:, u0:u1, c0:c1], in_=rows[:, u0:u1, c0:c1])
+
+        def load_rows(dst, src, g):
+            nc.sync.dma_start(out=dst[g][:], in_=src[g * G:(g + 1) * G, :].rearrange("(p t) c -> p t c", t=4))
+
+        def load_block(b, u0=0, u1=4):
+            g, h = divmod(b, NG)
+            load_loading(g, u0, u1, h * G, (h + 1) * G)
+
+        nc.vector.memset(x_sc[:].bitcast(I32), 0)
+        nc.vector.memset(v_sc_first[:].bitcast(I32), 0)
+        load_scales(nc.gpsimd, x_sc, x_scales, 0, D, (0, 1))
+        make_identity(nc, ident[:])
+        nc.gpsimd.memset(v_sc_rest[:].bitcast(I32), 0)
+
+        corr = {}
+        r_rows = {}
+        r_turned = {}
+        turned = {}
+        f_il = {}
+        y_il = {}
+        acc = {}
+        scaled_old = {}
+
+        def correlate(b, u):
+            g, h = divmod(b, NG)
+            out = bank(u, [P, G])
+            corr[b, u] = out
+            v_sc, c0 = (v_sc_first, 0) if g == 0 else (v_sc_rest, (g - 1) * G)
+            for k in range(NT):
+                nc.tensor.matmul_mx(
+                    out=out[:],
+                    lhsT=v_sb[g][:, k, 256 * u:256 * (u + 1)].bitcast(FP4X4),
+                    lhsT_scale=v_sc[:, k, c0 + P * u:c0 + P * (u + 1)],
+                    rhs=x_sb[h][:, k, :].bitcast(FP4X4),
+                    rhs_scale=x_sc[:, k, h * G:(h + 1) * G],
+                    start=(k == 0),
+                    stop=(k == NT - 1),
+                )
+
+        def add_loading(b, u):
+            g, h = divmod(b, NG)
+            r = stage.tile([P, G], BF16, name="r_rows", tag="r_rows", bufs=8, align_bytes=64)
+            r_rows[b, u] = r
+            nc.vector.tensor_tensor(
+                out=r[:].rearrange("p (a w e) -> p a w e", a=2, e=2),
+                in0=corr[b, u][:].rearrange("p (w a e) -> p a w e", a=2, e=2),
+                in1=load_sb[g][:, u, h * G:(h + 1) * G].rearrange("p (w a e) -> p a w e", a=2, e=2),
+                op=ALU.add,
+            )
+
+        def turn(b, u0, u1, n):
+            tb = bank(n, [P, 2, (u1 - u0) * P])
+            turned[b, u0] = tb
+            for u in range(u0, u1):
+                words = r_rows[b, u][:].bitcast(F32)
+                for a in range(2):
+                    nc.tensor.transpose(tb[:, a, (u - u0) * P:(u - u0 + 1) * P], words[:, a * P:(a + 1) * P], ident[:])
+
+        def copy_turned(b, u0, u1):
+            if u0 == 0:
+                r_turned[b] = stage.tile([P, 4 * G], BF16, name="r_turned", tag="r_turned", bufs=3, align_bytes=64)
+            dst = r_turned[b][:].bitcast(F32).rearrange("p (t x a) -> p t x a", t=4, a=2)
+            nc.scalar.copy(
+                out=dst[:, :, 32 * u0:32 * u1, :], in_=turned[b, u0][:].rearrange("p a (x t) -> p t x a", t=4)
+            )
+
+        def quantize_r(b, t0=0, t1=4):
+            nc.vector.quantize_mx(
+                out=r_codes[b][:, P * t0:P * t1].bitcast(FP8X4),
+                scales=r_scales[b][:, P * t0:P * t1],
+                in_=r_turned[b][:, G * t0:G * t1],
+            )
+
+        def interleave(engine_copy, dst, src):
+            engine_copy(out=dst.rearrange("p (c i t) -> p c t i", i=4, t=4), in_=src.rearrange("p t (c i) -> p c t i", i=4))
+
+        def interleave_filt(h):
+            f = stage.tile([P, 4 * C], BF16, name="f_il", tag="f_il", bufs=2, align_bytes=64)
+            f_il[h] = f
+            interleave(nc.scalar.copy, f[:], filt_sb[h][:])
+
+        def quantize_filt(h):
+            nc.vector.quantize_mx(out=f_codes[h][:].bitcast(FP8X4), scales=f_scales[h][:], in_=f_il[h][:])
+
+        def apply_filter(g, t, h, n):
+            if h == 0:
+                acc[g, t] = bank(n, [P, C])
+            b = g * NG + h
+            nc.tensor.matmul_mx(
+                out=acc[g, t][:],
+                lhsT=r_codes[b][:, P * t:P * (t + 1)].bitcast(FP8X4),
+                lhsT_scale=r_scales[b][:, P * t:P * (t + 1)],
+                rhs=f_codes[h][:].bitcast(FP8X4),
+                rhs_scale=f_scales[h][:],
+                start=(h == 0),
+                stop=(h == NG - 1),
+            )
+
+        def apply_all(g, t, n):
+            for h in range(NG):
+                apply_filter(g, t, h, n)
+
+        def scale_old(k):
+            g, s = divmod(k, 2)
+            so = stage.tile([P, 2, C], F32, name="scaled_old", tag="scaled_old", bufs=1, align_bytes=64)
+            scaled_old[k] = so
+            for tt in range(2):
+                nc.gpsimd.tensor_tensor(out=so[:, tt, :], in0=old_sb[g][:, 2 * s + tt, :], in1=beta_all[:], op=ALU.mult)
+
+        def make_base(g, t):
+            nc.vector.scalar_tensor_tensor(
+                out=y_sb[g][:, t, :], in0=rhs_sb[g][:, t, :], scalar=step_pos[:, 4 * g + t:4 * g + t + 1],
+                in1=scaled_old[2 * g + t // 2][:, t % 2, :], op0=ALU.mult, op1=ALU.add,
+            )
+
+        def finish(g, t, c0=0, c1=C):
+            nc.vector.scalar_tensor_tensor(
+                out=y_sb[g][:, t, c0:c1], in0=acc[g, t][:, c0:c1], scalar=step_neg[:, 4 * g + t:4 * g + t + 1],
+                in1=y_sb[g][:, t, c0:c1], op0=ALU.mult, op1=ALU.add,
+            )
+
+        def store_y(g, t0=0, t1=4, c0=0, c1=C):
+            rows = out_0[g * G:(g + 1) * G, :].rearrange("(p t) c -> p t c", t=4)
+            nc.sync.dma_start(out=rows[:, t0:t1, c0:c1], in_=y_sb[g][:, t0:t1, c0:c1])
+
+        def interleave_y(g, on_vector, c0=0, c1=C):
+            engine_copy = nc.vector.tensor_copy if on_vector else nc.scalar.copy
+            if c0 == 0:
+                y_il[g] = stage.tile([P, 4 * C], BF16, name="y_il", tag="y_il", bufs=2, align_bytes=64)
+            interleave(engine_copy, y_il[g][:, 4 * c0:4 * c1], y_sb[g][:, :, c0:c1])
+
+        def quantize_y(g, c0=0, c1=C):
+            nc.vector.quantize_mx(
+                out=y_codes[g][:, c0:c1].bitcast(FP8X4), scales=y_scales[:, g, c0:c1], in_=y_il[g][:, 4 * c0:4 * c1]
+            )
+            words = out_1[g].rearrange("p m t -> p (m t)").bitcast(I32)
+            nc.sync.dma_start(out=words[:, c0:c1], in_=y_codes[g][:, c0:c1].bitcast(I32))
+
+        def spread_beta():
+            nc.scalar.copy(out=beta_col[:], in_=beta_bf[:])
+            nc.scalar.copy(out=step_pos[:], in_=step_bf[:].rearrange("p g t -> p (g t)"))
+            nc.gpsimd.tensor_scalar(
+                out=step_neg[:], in0=step_bf[:].rearrange("p g t -> p (g t)"),
+                scalar1=-1.0, scalar2=0.0, op0=ALU.mult, op1=ALU.add,
+            )
+            bb = bank(6, [P, 4, P])
+            for q in range(4):
+                nc.tensor.transpose(bb[:, q, :], beta_col[:, q:q + 1].to_broadcast([P, P]), ident[:])
+            nc.scalar.copy(out=beta_all[:].rearrange("p (c q) -> p c q", q=4), in_=bb[:].rearrange("p q c -> p c q"))
+
+        def store_scales():
+            scale_rows = out_2.bitcast(I32)
+            for q in range(4):
+                queue = nc.sync if q < 2 else nc.scalar
+                queue.dma_start(
+                    out=scale_rows[:, 4 * q:4 * q + 4, :].rearrange("g r w -> r g w"),
+                    in_=y_scales[32 * q:32 * q + 4, :, :].bitcast(I32),
+                )
+
+        def load_small():
+            nc.sync.dma_start(out=beta_bf[:], in_=beta.rearrange("(p q) -> p q", q=4))
+            nc.sync.dma_start(out=step_bf[:], in_=step.rearrange("(g p t) -> p g t", p=P, t=4))
+
+        def load_head():
+            load_words(x_sb[0], x_words, 0)
+            load_words(v_sb[0], v_words, 0)
+            load_scales(nc.sync, x_sc, x_scales, 0, D, (2, 3))
+            load_scales(nc.sync, v_sc_first, v_scales, 0, G, range(4))
+
+        actions = {
+            "head": load_head,
+            "lsmall": load_small,
+            "lx": lambda h: load_words(x_sb[h], x_words, h),
+            "lv": lambda g: load_words(v_sb[g], v_words, g),
+            "lvs": lambda: load_scales(nc.sync, v_sc_rest, v_scales, G, D, range(4)),
+            "lb": load_block,
+            "lf": lambda h: load_rows(filt_sb, filt, h),
+            "lo": lambda g: load_rows(old_sb, p_old, g),
+            "lr": lambda g: load_rows(rhs_sb, rhs, g),
+            "mm": correlate,
+            "add": add_loading,
+            "T": turn,
+            "C": copy_turned,
+            "Q": quantize_r,
+            "F": interleave_filt,
+            "Qf": quantize_filt,
+            "S": apply_filter,
+            "beta": spread_beta,
+            "B1": scale_old,
+            "B2": make_base,
+            "Y": finish,
+            "st": store_y,
+            "I": interleave_y,
+            "Qy": quantize_y,
+            "ss": store_scales,
+        }
+        for token in ORDER:
+            actions[token[0]](*token[1:])

@@ -11,6 +11,7 @@ U8 = mybir.dt.uint8
 FP4X4 = mybir.dt.float4_e2m1fn_x4
 FP8X4 = mybir.dt.float8_e4m3fn_x4
 ALU = mybir.AluOpType
+ACT = mybir.ActivationFunctionType
 
 T, D, C = 1024, 1536, 512
 FLOPS = 2 * T * D * D + 2 * D * D * C
@@ -22,243 +23,268 @@ NT = T // G
 NB = NG * NG
 
 ORDER = [
-    ("head",),
-    ("lf", 0),
-    ("lb", 0, 0, 2),
-    ("mm", 0, 0),
+    ("lvf",),
+    ("ms", 0),
+    ("id",),
     ("lsmall",),
-    ("add", 0, 0),
-    ("mm", 0, 1),
-    ("lb", 0, 2, 4),
-    ("mm", 0, 2),
-    ("add", 0, 1),
-    ("F", 0),
-    ("lx", 1),
-    ("mm", 0, 3),
-    ("mm", 1, 0),
-    ("add", 0, 2),
-    ("lb", 1),
-    ("mm", 1, 1),
-    ("T", 0, 0, 2, 4),
-    ("lx", 2),
-    ("add", 0, 3),
+    ("lv", 0),
+    ("lsv", 2),
+    ("lsv", 0),
+    ("lsv", 3),
     ("lo", 0),
-    ("lb", 2),
-    ("lvs",),
-    ("add", 1, 0),
+    ("lx", 0),
     ("beta",),
-    ("C", 0, 0, 2),
-    ("T", 0, 2, 4, 5),
-    ("add", 1, 1),
+    ("ms", 2),
+    ("ms", 1),
+    ("lsx", 2),
+    ("lsx", 3),
+    ("lsx", 0),
+    ("lsv", 1),
+    ("lsx", 1),
+    ("lb", 0, 0, 2),
+    ("warm", 14),
     ("lr", 0),
+    ("mm", 0, 0),
+    ("A2", 0, 0),
+    ("mm", 0, 1),
+    ("lx", 1),
+    ("mm", 0, 2),
+    ("B1", 0),
+    ("add", 0, 0),
+    ("mm", 0, 3),
+    ("lb", 0, 2, 4),
+    ("lb", 1),
+    ("P2", 0, 0),
+    ("add", 0, 1),
+    ("B2", 0, 1),
+    ("T", 0, 0, 2, 4),
+    ("add", 0, 2),
+    ("mm", 1, 0),
+    ("lx", 2),
+    ("mm", 1, 1),
+    ("add", 0, 3),
+    ("C", 0, 0, 2),
+    ("add", 1, 0),
     ("mm", 1, 2),
-    ("Qf", 0),
+    ("add", 1, 1),
+    ("add", 1, 2),
     ("mm", 1, 3),
+    ("lb", 2),
+    ("B1", 1),
+    ("lf", 0),
+    ("add", 1, 3),
+    ("T", 0, 2, 4, 5),
+    ("B2", 0, 3),
+    ("T", 1, 0, 2, 4),
     ("lv", 1),
     ("mm", 2, 0),
-    ("add", 1, 2),
-    ("lf", 1),
-    ("add", 1, 3),
-    ("mm", 2, 1),
     ("C", 0, 2, 4),
     ("add", 2, 0),
-    ("T", 1, 0, 2, 4),
-    ("T", 1, 2, 4, 5),
-    ("B1", 0),
     ("C", 1, 0, 2),
-    ("C", 1, 2, 4),
-    ("add", 2, 1),
-    ("lb", 3),
+    ("A2", 0, 2),
+    ("lvs",),
+    ("mm", 2, 1),
     ("mm", 2, 2),
-    ("Q", 0),
-    ("lf", 2),
-    ("B2", 0, 0),
-    ("Q", 1),
-    ("add", 2, 2),
+    ("add", 2, 1),
     ("mm", 2, 3),
+    ("lb", 3),
     ("mm", 3, 0),
+    ("lf", 1),
+    ("T", 1, 2, 4, 5),
+    ("add", 2, 2),
     ("T", 2, 0, 2, 4),
     ("mm", 3, 1),
-    ("mm", 3, 2),
-    ("B2", 0, 1),
-    ("S", 0, 0, 0, 6),
     ("add", 2, 3),
-    ("F", 1),
+    ("Q", 0),
+    ("F", 0),
+    ("C", 1, 2, 4),
     ("add", 3, 0),
-    ("add", 3, 1),
-    ("lb", 4),
-    ("mm", 3, 3),
-    ("lv", 2),
-    ("B1", 1),
-    ("lb", 5),
-    ("lo", 1),
+    ("Qf", 0),
+    ("mm", 3, 2),
+    ("P2", 0, 2),
     ("C", 2, 0, 2),
+    ("mm", 3, 3),
+    ("Q", 1),
     ("mm", 4, 0),
-    ("mm", 4, 1),
-    ("F", 2),
+    ("lo", 1),
+    ("lb", 4),
+    ("F", 1),
+    ("add", 3, 1),
     ("T", 2, 2, 4, 5),
     ("add", 3, 2),
-    ("mm", 4, 2),
-    ("S", 0, 1, 0, 7),
+    ("lf", 2),
     ("add", 3, 3),
-    ("mm", 4, 3),
-    ("Qf", 1),
-    ("B2", 0, 2),
-    ("add", 4, 0),
-    ("add", 4, 1),
-    ("T", 3, 0, 2, 4),
-    ("C", 2, 2, 4),
-    ("T", 3, 2, 4, 5),
-    ("Qf", 2),
-    ("mm", 5, 0),
-    ("lr", 2),
-    ("add", 4, 2),
-    ("B2", 0, 3),
-    ("Q", 2),
-    ("B1", 2),
-    ("S", 0, 1, 1, 7),
-    ("mm", 5, 1),
-    ("mm", 5, 2),
     ("lr", 1),
-    ("C", 3, 0, 2),
-    ("C", 3, 2, 4),
-    ("add", 4, 3),
-    ("S", 0, 1, 2, 7),
-    ("S", 0, 0, 1, 6),
-    ("add", 5, 0),
-    ("add", 5, 1),
-    ("mm", 5, 3),
-    ("S", 0, 0, 2, 6),
-    ("add", 5, 2),
-    ("add", 5, 3),
-    ("Y", 0, 0),
-    ("Q", 3),
-    ("B2", 1, 0),
+    ("add", 4, 0),
+    ("T", 3, 0, 2, 4),
+    ("mm", 4, 1),
+    ("C", 2, 2, 4),
+    ("lv", 2),
+    ("lb", 5),
+    ("mm", 4, 2),
+    ("add", 4, 1),
+    ("mm", 4, 3),
+    ("B1", 2),
+    ("Qf", 1),
+    ("mm", 5, 0),
+    ("add", 4, 2),
+    ("lr", 2),
     ("lb", 6),
+    ("C", 3, 0, 2),
+    ("Q", 2),
+    ("T", 3, 2, 4, 5),
     ("T", 4, 0, 2, 4),
-    ("T", 4, 2, 4, 5),
+    ("add", 4, 3),
+    ("F", 2),
     ("B2", 1, 1),
+    ("Qf", 2),
+    ("S", 0, 1, 0, 7),
+    ("lo", 2),
+    ("lb", 7),
+    ("mm", 5, 1),
+    ("A2", 1, 0),
+    ("S", 0, 0, 0, 6),
+    ("add", 5, 0),
+    ("S", 0, 0, 1, 6),
+    ("mm", 5, 2),
+    ("mm", 5, 3),
+    ("add", 5, 1),
+    ("C", 3, 2, 4),
+    ("S", 0, 0, 2, 6),
+    ("S", 0, 1, 1, 7),
+    ("T", 4, 2, 4, 5),
     ("C", 4, 0, 2),
-    ("C", 4, 2, 4),
+    ("T", 5, 0, 2, 4),
+    ("Y", 0, 0),
+    ("add", 5, 2),
+    ("lb", 8),
+    ("S", 0, 1, 2, 7),
+    ("add", 5, 3),
+    ("P2", 1, 0),
+    ("Y", 0, 1),
+    ("S", 0, 2, 0, 6),
     ("mm", 6, 0),
     ("mm", 6, 1),
-    ("T", 5, 0, 2, 4),
-    ("T", 5, 2, 4, 5),
-    ("Y", 0, 1),
     ("add", 6, 0),
-    ("S", 0, 2, 0, 6),
-    ("mm", 6, 2),
-    ("S", 0, 2, 1, 6),
-    ("lb", 7),
-    ("add", 6, 1),
     ("B1", 3),
-    ("lo", 2),
+    ("S", 0, 2, 1, 6),
+    ("mm", 6, 2),
+    ("S", 0, 3, 0, 7),
+    ("C", 4, 2, 4),
+    ("add", 6, 1),
     ("C", 5, 0, 2),
+    ("A2", 1, 2),
+    ("add", 6, 2),
+    ("Q", 3),
+    ("B2", 1, 3),
+    ("Q", 4),
+    ("P2", 1, 2),
     ("mm", 6, 3),
     ("mm", 7, 0),
     ("S", 0, 2, 2, 6),
-    ("add", 6, 2),
-    ("add", 6, 3),
-    ("S", 0, 3, 0, 7),
-    ("lb", 8),
-    ("C", 5, 2, 4),
-    ("add", 7, 0),
-    ("S", 0, 3, 1, 7),
-    ("B2", 1, 2),
-    ("B2", 1, 3),
-    ("mm", 7, 1),
-    ("S", 0, 3, 2, 7),
-    ("Q", 4),
-    ("Y", 0, 2),
+    ("T", 5, 2, 4, 5),
     ("T", 6, 0, 2, 4),
-    ("T", 6, 2, 4, 5),
+    ("S", 0, 3, 1, 7),
+    ("mm", 7, 1),
+    ("st", 0, 0, 2),
+    ("B1", 4),
+    ("Y", 0, 2),
+    ("S", 0, 3, 2, 7),
+    ("C", 5, 2, 4),
+    ("mm", 7, 2),
+    ("add", 6, 3),
+    ("add", 7, 0),
     ("add", 7, 1),
     ("Y", 0, 3),
-    ("mm", 7, 2),
-    ("add", 7, 2),
     ("mm", 7, 3),
-    ("mm", 8, 0),
-    ("add", 7, 3),
     ("C", 6, 0, 2),
-    ("S", 1, 0, 0, 6),
-    ("S", 1, 1, 0, 7),
-    ("Q", 5),
-    ("mm", 8, 1),
+    ("T", 6, 2, 4, 5),
+    ("add", 7, 2),
+    ("A2", 2, 0),
     ("C", 6, 2, 4),
-    ("B1", 4),
-    ("mm", 8, 2),
-    ("S", 1, 0, 1, 6),
-    ("S", 1, 0, 2, 6),
-    ("S", 1, 1, 1, 7),
-    ("add", 8, 0),
-    ("B2", 2, 0),
-    ("S", 1, 1, 2, 7),
+    ("add", 7, 3),
+    ("P2", 2, 0),
+    ("T", 7, 0, 2, 4),
+    ("mm", 8, 0),
+    ("Q", 5),
+    ("S", 1, 0, 0, 6),
+    ("mm", 8, 1),
     ("I", 0, 0),
+    ("B2", 2, 1),
+    ("B1", 5),
+    ("S", 1, 1, 0, 7),
+    ("S", 1, 0, 1, 6),
+    ("C", 7, 0, 2),
+    ("S", 1, 0, 2, 6),
     ("Q", 6),
     ("Y", 1, 0),
-    ("T", 7, 0, 2, 4),
-    ("B2", 2, 1),
-    ("Y", 1, 1),
-    ("st", 1, 0, 2),
-    ("T", 7, 2, 4, 5),
+    ("mm", 8, 2),
+    ("S", 1, 1, 1, 7),
+    ("S", 1, 1, 2, 7),
     ("mm", 8, 3),
+    ("add", 8, 0),
     ("add", 8, 1),
+    ("st", 0, 2, 4),
+    ("Y", 1, 1),
     ("S", 1, 2, 0, 6),
-    ("C", 7, 0, 2),
-    ("C", 7, 2, 4),
     ("S", 1, 2, 1, 6),
-    ("add", 8, 2),
-    ("add", 8, 3),
     ("S", 1, 2, 2, 6),
+    ("T", 7, 2, 4, 5),
+    ("add", 8, 2),
+    ("T", 8, 0, 2, 4),
     ("S", 1, 3, 0, 7),
     ("S", 1, 3, 1, 7),
     ("S", 1, 3, 2, 7),
-    ("T", 8, 0, 2, 4),
-    ("T", 8, 2, 3, 5),
-    ("B1", 5),
-    ("Y", 1, 2),
-    ("T", 8, 3, 4, 6),
-    ("S", 2, 0, 0, 0),
-    ("C", 8, 0, 2),
-    ("S", 2, 3, 0, 3),
-    ("C", 8, 2, 3),
-    ("st", 0, 0, 2),
-    ("C", 8, 3, 4),
-    ("Y", 1, 3),
-    ("Qy", 0),
-    ("Q", 7),
-    ("I", 1, 0),
-    ("Q", 8, 0, 2),
-    ("B2", 2, 2),
     ("S", 2, 1, 0, 1),
+    ("add", 8, 3),
+    ("S", 2, 0, 0, 0),
+    ("Y", 1, 2),
+    ("A2", 2, 2),
+    ("C", 7, 2, 4),
+    ("T", 8, 2, 3, 5),
+    ("Q", 7),
+    ("T", 8, 3, 4, 6),
+    ("C", 8, 0, 2),
+    ("Y", 1, 3),
+    ("st", 1, 0, 2),
+    ("Qy", 0),
+    ("C", 8, 2, 3),
+    ("C", 8, 3, 4),
+    ("Q", 8, 0, 2),
+    ("S", 2, 3, 0, 3),
     ("S", 2, 2, 0, 2),
-    ("S", 2, 1, 1, 1),
-    ("S", 2, 0, 1, 0),
     ("S", 2, 3, 1, 3),
-    ("S", 2, 0, 2, 0),
-    ("st", 0, 2, 4),
+    ("S", 2, 0, 1, 0),
+    ("S", 2, 2, 1, 2),
+    ("P2", 2, 2),
+    ("S", 2, 1, 1, 1),
     ("Q", 8, 2, 4),
+    ("st", 1, 2, 4),
+    ("S", 2, 0, 2, 0),
+    ("I", 1, 0),
     ("B2", 2, 3),
     ("S", 2, 1, 2, 1),
-    ("S", 2, 3, 2, 3),
-    ("st", 1, 2, 4),
-    ("Y", 2, 0, 0, 256),
-    ("S", 2, 2, 1, 2),
     ("S", 2, 2, 2, 2),
-    ("Y", 2, 1, 0, 256),
+    ("S", 2, 3, 2, 3),
+    ("Y", 2, 0, 0),
+    ("sc", 0),
+    ("Y", 2, 1, 0),
+    ("Y", 2, 2, 0),
+    ("Y", 2, 3, 0),
+    ("Y", 2, 0, 1),
+    ("st", 2, 0, 4, 0),
+    ("Y", 2, 1, 1),
+    ("Y", 2, 2, 1),
+    ("Y", 2, 3, 1),
+    ("st", 2, 0, 4, 1),
     ("Qy", 1),
-    ("Y", 2, 2, 0, 256),
-    ("Y", 2, 3, 0, 256),
-    ("Y", 2, 0, 256, 512),
-    ("Y", 2, 1, 256, 512),
-    ("I", 2, 0, 0, 256),
-    ("st", 2, 0, 4, 0, 256),
-    ("Y", 2, 2, 256, 512),
-    ("Y", 2, 3, 256, 512),
-    ("I", 2, 1, 256, 512),
-    ("st", 2, 0, 4, 256, 512),
-    ("Qy", 2, 0, 256),
-    ("Qy", 2, 256, 512),
+    ("I", 2, 0, 0),
+    ("I", 2, 1, 1),
+    ("sc", 1),
+    ("Qy", 2, 0),
+    ("sc", 2, 0),
+    ("Qy", 2, 1),
+    ("sc", 2, 1),
     ("ss",),
 ]
 
@@ -276,16 +302,21 @@ def tile_wpe_search_direction_k5_kernel(
         def kept(name, shape, dtype):
             return keep.tile(shape, dtype, name=name, align_bytes=64)
 
+        v_first = kept("v_first", [P, NT, 2 * P], U8)
         v_sb = [kept("v_sb%d" % g, [P, NT, 2 * G], U8) for g in range(NG)]
+        warm_in = kept("warm_in", [P, 4 * P], BF16)
+        warm_codes = kept("warm_codes", [P, P], U32)
+        warm_scales = kept("warm_scales", [P, P], U8)
         x_sb = [kept("x_sb%d" % g, [P, NT, 2 * G], U8) for g in range(NG)]
         v_sc_first = kept("v_sc_first", [P, NT, G], U8)
         v_sc_rest = kept("v_sc_rest", [P, NT, D - G], U8)
         x_sc = kept("x_sc", [P, NT, D], U8)
-        load_sb = [kept("load_sb%d" % g, [P, 4, D], BF16) for g in range(NG)]
+        load_sb = [kept("load_sb%d" % b, [P, 4, G], BF16) for b in range(NB)]
         filt_sb = [kept("filt_sb%d" % g, [P, 4, C], BF16) for g in range(NG)]
         rhs_sb = [kept("rhs_sb%d" % g, [P, 4, C], BF16) for g in range(NG)]
         old_sb = [kept("old_sb%d" % g, [P, 4, C], BF16) for g in range(NG)]
-        y_sb = [kept("y_sb%d" % g, [P, 4, C], F32) for g in range(NG)]
+        parts = [1, 1, 2]
+        y_sb = [kept("y_sb%d" % g, [P, parts[g], 4, C // parts[g]], F32) for g in range(NG)]
         r_codes = [kept("r_codes%d" % b, [P, G], U32) for b in range(NB)]
         r_scales = [kept("r_scales%d" % b, [P, G], U8) for b in range(NB)]
         f_codes = [kept("f_codes%d" % g, [P, C], U32) for g in range(NG)]
@@ -303,9 +334,9 @@ def tile_wpe_search_direction_k5_kernel(
         def bank(n, shape):
             return psum.tile(shape, F32, name="bank%d" % n, tag="bank%d" % n)
 
-        def load_words(dst, src, g):
+        def load_words(dst, src, c0, c1):
             view = src.bitcast(I32).rearrange("k p w -> p k w")
-            nc.sync.dma_start(out=dst[:].bitcast(I32), in_=view[:, :, g * 256:(g + 1) * 256])
+            nc.sync.dma_start(out=dst.bitcast(I32), in_=view[:, :, c0 // 2:c1 // 2])
 
         def load_scales(queue, dst, src, c0, c1, quadrants):
             view = src.bitcast(I32)
@@ -313,22 +344,14 @@ def tile_wpe_search_direction_k5_kernel(
                 rows = view[:, 4 * q:4 * q + 4, c0 // 4:c1 // 4].rearrange("k r w -> r k w")
                 queue.dma_start(out=dst[32 * q:32 * q + 4, :, :].bitcast(I32), in_=rows)
 
-        def load_loading(g, u0, u1, c0, c1):
-            rows = loading[g * G:(g + 1) * G, :].rearrange("(u p) j -> p u j", p=P)
-            nc.sync.dma_start(out=load_sb[g][:, u0:u1, c0:c1], in_=rows[:, u0:u1, c0:c1])
-
         def load_rows(dst, src, g):
             nc.sync.dma_start(out=dst[g][:], in_=src[g * G:(g + 1) * G, :].rearrange("(p t) c -> p t c", t=4))
 
         def load_block(b, u0=0, u1=4):
             g, h = divmod(b, NG)
-            load_loading(g, u0, u1, h * G, (h + 1) * G)
+            rows = loading[g * G:(g + 1) * G, h * G:(h + 1) * G].rearrange("(u p) j -> p u j", p=P)
+            nc.sync.dma_start(out=load_sb[b][:, u0:u1, :], in_=rows[:, u0:u1, :])
 
-        nc.vector.memset(x_sc[:].bitcast(I32), 0)
-        nc.vector.memset(v_sc_first[:].bitcast(I32), 0)
-        load_scales(nc.gpsimd, x_sc, x_scales, 0, D, (0, 1))
-        make_identity(nc, ident[:])
-        nc.gpsimd.memset(v_sc_rest[:].bitcast(I32), 0)
 
         corr = {}
         r_rows = {}
@@ -347,7 +370,7 @@ def tile_wpe_search_direction_k5_kernel(
             for k in range(NT):
                 nc.tensor.matmul_mx(
                     out=out[:],
-                    lhsT=v_sb[g][:, k, 256 * u:256 * (u + 1)].bitcast(FP4X4),
+                    lhsT=(v_first[:, k, :] if (g, u) == (0, 0) else v_sb[g][:, k, 256 * u:256 * (u + 1)]).bitcast(FP4X4),
                     lhsT_scale=v_sc[:, k, c0 + P * u:c0 + P * (u + 1)],
                     rhs=x_sb[h][:, k, :].bitcast(FP4X4),
                     rhs_scale=x_sc[:, k, h * G:(h + 1) * G],
@@ -356,13 +379,12 @@ def tile_wpe_search_direction_k5_kernel(
                 )
 
         def add_loading(b, u):
-            g, h = divmod(b, NG)
             r = stage.tile([P, G], BF16, name="r_rows", tag="r_rows", bufs=8, align_bytes=64)
             r_rows[b, u] = r
             nc.vector.tensor_tensor(
                 out=r[:].rearrange("p (a w e) -> p a w e", a=2, e=2),
                 in0=corr[b, u][:].rearrange("p (w a e) -> p a w e", a=2, e=2),
-                in1=load_sb[g][:, u, h * G:(h + 1) * G].rearrange("p (w a e) -> p a w e", a=2, e=2),
+                in1=load_sb[b][:, u, :].rearrange("p (w a e) -> p a w e", a=2, e=2),
                 op=ALU.add,
             )
 
@@ -427,30 +449,45 @@ def tile_wpe_search_direction_k5_kernel(
 
         def make_base(g, t):
             nc.vector.scalar_tensor_tensor(
-                out=y_sb[g][:, t, :], in0=rhs_sb[g][:, t, :], scalar=step_pos[:, 4 * g + t:4 * g + t + 1],
-                in1=scaled_old[2 * g + t // 2][:, t % 2, :], op0=ALU.mult, op1=ALU.add,
+                out=y_sb[g][:, :, t, :],
+                in0=rhs_sb[g][:, t, :].rearrange("p (s c) -> p s c", s=parts[g]),
+                scalar=step_pos[:, 4 * g + t:4 * g + t + 1],
+                in1=scaled_old[2 * g + t // 2][:, t % 2, :].rearrange("p (s c) -> p s c", s=parts[g]),
+                op0=ALU.mult,
+                op1=ALU.add,
             )
 
-        def finish(g, t, c0=0, c1=C):
+        def columns(g, s):
+            width = C // parts[g]
+            return s * width, (s + 1) * width
+
+        def finish(g, t, s=0):
+            c0, c1 = columns(g, s)
             nc.vector.scalar_tensor_tensor(
-                out=y_sb[g][:, t, c0:c1], in0=acc[g, t][:, c0:c1], scalar=step_neg[:, 4 * g + t:4 * g + t + 1],
-                in1=y_sb[g][:, t, c0:c1], op0=ALU.mult, op1=ALU.add,
+                out=y_sb[g][:, s, t, :], in0=acc[g, t][:, c0:c1], scalar=step_neg[:, 4 * g + t:4 * g + t + 1],
+                in1=y_sb[g][:, s, t, :], op0=ALU.mult, op1=ALU.add,
             )
 
-        def store_y(g, t0=0, t1=4, c0=0, c1=C):
+        def store_y(g, t0, t1, s=0):
+            c0, c1 = columns(g, s)
             rows = out_0[g * G:(g + 1) * G, :].rearrange("(p t) c -> p t c", t=4)
-            nc.sync.dma_start(out=rows[:, t0:t1, c0:c1], in_=y_sb[g][:, t0:t1, c0:c1])
+            nc.sync.dma_start(out=rows[:, t0:t1, c0:c1], in_=y_sb[g][:, s, t0:t1, :])
 
-        def interleave_y(g, on_vector, c0=0, c1=C):
+        def interleave_y(g, on_vector, s=0):
+            c0, c1 = columns(g, s)
             engine_copy = nc.vector.tensor_copy if on_vector else nc.scalar.copy
-            if c0 == 0:
+            if s == 0:
                 y_il[g] = stage.tile([P, 4 * C], BF16, name="y_il", tag="y_il", bufs=2, align_bytes=64)
-            interleave(engine_copy, y_il[g][:, 4 * c0:4 * c1], y_sb[g][:, :, c0:c1])
+            interleave(engine_copy, y_il[g][:, 4 * c0:4 * c1], y_sb[g][:, s, :, :])
 
-        def quantize_y(g, c0=0, c1=C):
+        def quantize_y(g, s=0):
+            c0, c1 = columns(g, s)
             nc.vector.quantize_mx(
                 out=y_codes[g][:, c0:c1].bitcast(FP8X4), scales=y_scales[:, g, c0:c1], in_=y_il[g][:, 4 * c0:4 * c1]
             )
+
+        def store_codes(g, s=0):
+            c0, c1 = columns(g, s)
             words = out_1[g].rearrange("p m t -> p (m t)").bitcast(I32)
             nc.sync.dma_start(out=words[:, c0:c1], in_=y_codes[g][:, c0:c1].bitcast(I32))
 
@@ -479,17 +516,48 @@ def tile_wpe_search_direction_k5_kernel(
             nc.sync.dma_start(out=beta_bf[:], in_=beta.rearrange("(p q) -> p q", q=4))
             nc.sync.dma_start(out=step_bf[:], in_=step.rearrange("(g p t) -> p g t", p=P, t=4))
 
-        def load_head():
-            load_words(x_sb[0], x_words, 0)
-            load_words(v_sb[0], v_words, 0)
-            load_scales(nc.sync, x_sc, x_scales, 0, D, (2, 3))
-            load_scales(nc.sync, v_sc_first, v_scales, 0, G, range(4))
+        def load_v(g):
+            skip = P if g == 0 else 0
+            load_words(v_sb[g][:, :, 2 * skip:], v_words, g * G + skip, (g + 1) * G)
+
+        def warm_up(passes):
+            nc.vector.memset(warm_in[:], 1.0)
+            nc.vector.quantize_mx(out=warm_codes[:].bitcast(FP8X4), scales=warm_scales[:], in_=warm_in[:])
+            out = bank(7, [P, P])
+            for n in range(passes):
+                nc.tensor.matmul_mx(
+                    out=out[:], lhsT=warm_codes[:].bitcast(FP8X4), lhsT_scale=warm_scales[:],
+                    rhs=warm_codes[:].bitcast(FP8X4), rhs_scale=warm_scales[:], start=True, stop=True,
+                )
+
+        def scale_rhs(g, t):
+            nc.scalar.activation(
+                out=y_sb[g][:, :, t, :],
+                in_=rhs_sb[g][:, t, :].rearrange("p (s c) -> p s c", s=parts[g]),
+                func=ACT.Copy,
+                scale=step_pos[:, 4 * g + t:4 * g + t + 1],
+            )
+
+        def add_old(g, t):
+            nc.gpsimd.tensor_tensor(
+                out=y_sb[g][:, :, t, :],
+                in0=y_sb[g][:, :, t, :],
+                in1=scaled_old[2 * g + t // 2][:, t % 2, :].rearrange("p (s c) -> p s c", s=parts[g]),
+                op=ALU.add,
+            )
 
         actions = {
-            "head": load_head,
+            "ms": lambda n: nc.vector.memset((v_sc_first, x_sc, v_sc_rest)[n][:].bitcast(I32), 0),
+            "id": lambda: make_identity(nc, ident[:]),
+            "warm": warm_up,
+            "A2": scale_rhs,
+            "P2": add_old,
+            "lvf": lambda: load_words(v_first[:], v_words, 0, P),
+            "lsv": lambda q: load_scales(nc.sync, v_sc_first, v_scales, 0, G, (q,)),
+            "lsx": lambda q: load_scales(nc.sync, x_sc, x_scales, 0, D, (q,)),
             "lsmall": load_small,
-            "lx": lambda h: load_words(x_sb[h], x_words, h),
-            "lv": lambda g: load_words(v_sb[g], v_words, g),
+            "lx": lambda h: load_words(x_sb[h][:], x_words, h * G, (h + 1) * G),
+            "lv": load_v,
             "lvs": lambda: load_scales(nc.sync, v_sc_rest, v_scales, G, D, range(4)),
             "lb": load_block,
             "lf": lambda h: load_rows(filt_sb, filt, h),
@@ -510,6 +578,7 @@ def tile_wpe_search_direction_k5_kernel(
             "st": store_y,
             "I": interleave_y,
             "Qy": quantize_y,
+            "sc": store_codes,
             "ss": store_scales,
         }
         for token in ORDER:

@@ -21,271 +21,279 @@ G = 512
 NG = D // G
 NT = T // G
 NB = NG * NG
+XF = 512
 
 ORDER = [
-    ("lvf",),
-    ("ms", 0),
     ("id",),
-    ("lsmall",),
-    ("lv", 0),
-    ("lsv", 2),
-    ("lsv", 0),
-    ("lsv", 3),
-    ("lo", 0),
-    ("lx", 0),
-    ("beta",),
-    ("ms", 2),
+    ("ms", 0),
     ("ms", 1),
+    ("ms", 3),
+    ("ms", 2),
+    ("lr", 0, 0, 2),
+    ("lsmall",),
+    ("lb", 0, 0, 512),
+    ("lvf",),
+    ("lsv", 3),
     ("lsx", 2),
-    ("lsx", 3),
-    ("lsx", 0),
-    ("lsv", 1),
-    ("lsx", 1),
-    ("lb", 0, 0, 2),
-    ("warm", 14),
-    ("lr", 0),
-    ("mm", 0, 0),
-    ("A2", 0, 0),
-    ("mm", 0, 1),
     ("lx", 1),
-    ("mm", 0, 2),
-    ("B1", 0),
-    ("add", 0, 0),
-    ("mm", 0, 3),
-    ("lb", 0, 2, 4),
+    ("lsv", 0),
+    ("lsx", 0),
+    ("lsv", 2),
+    ("lsx", 3),
+    ("lsx", 1),
+    ("lo", 0, 0, 2),
+    ("lx", 0),
+    ("lsv", 1),
+    ("lxs",),
+    ("lv", 0),
+    ("lb", 0, 512, 1536),
     ("lb", 1),
-    ("P2", 0, 0),
-    ("add", 0, 1),
-    ("B2", 0, 1),
-    ("T", 0, 0, 2, 4),
-    ("add", 0, 2),
-    ("mm", 1, 0),
-    ("lx", 2),
-    ("mm", 1, 1),
-    ("add", 0, 3),
-    ("C", 0, 0, 2),
-    ("add", 1, 0),
-    ("mm", 1, 2),
-    ("add", 1, 1),
-    ("add", 1, 2),
-    ("mm", 1, 3),
-    ("lb", 2),
-    ("B1", 1),
     ("lf", 0),
-    ("add", 1, 3),
-    ("T", 0, 2, 4, 5),
-    ("B2", 0, 3),
-    ("T", 1, 0, 2, 4),
-    ("lv", 1),
-    ("mm", 2, 0),
-    ("C", 0, 2, 4),
-    ("add", 2, 0),
-    ("C", 1, 0, 2),
-    ("A2", 0, 2),
+    ("lo", 0, 2, 4),
+    ("lb", 2),
     ("lvs",),
-    ("mm", 2, 1),
-    ("mm", 2, 2),
-    ("add", 2, 1),
-    ("mm", 2, 3),
     ("lb", 3),
-    ("mm", 3, 0),
-    ("lf", 1),
-    ("T", 1, 2, 4, 5),
-    ("add", 2, 2),
-    ("T", 2, 0, 2, 4),
-    ("mm", 3, 1),
-    ("add", 2, 3),
-    ("Q", 0),
-    ("F", 0),
-    ("C", 1, 2, 4),
-    ("add", 3, 0),
-    ("Qf", 0),
-    ("mm", 3, 2),
-    ("P2", 0, 2),
-    ("C", 2, 0, 2),
-    ("mm", 3, 3),
-    ("Q", 1),
-    ("mm", 4, 0),
-    ("lo", 1),
+    ("lr", 0, 2, 4),
+    ("lv", 1),
     ("lb", 4),
-    ("F", 1),
-    ("add", 3, 1),
-    ("T", 2, 2, 4, 5),
-    ("add", 3, 2),
-    ("lf", 2),
-    ("add", 3, 3),
-    ("lr", 1),
-    ("add", 4, 0),
-    ("T", 3, 0, 2, 4),
-    ("mm", 4, 1),
-    ("C", 2, 2, 4),
-    ("lv", 2),
+    ("lo", 1),
+    ("lf", 1),
     ("lb", 5),
-    ("mm", 4, 2),
-    ("add", 4, 1),
-    ("mm", 4, 3),
-    ("B1", 2),
-    ("Qf", 1),
-    ("mm", 5, 0),
-    ("add", 4, 2),
-    ("lr", 2),
+    ("lr", 1),
+    ("lf", 2),
     ("lb", 6),
-    ("C", 3, 0, 2),
-    ("Q", 2),
-    ("T", 3, 2, 4, 5),
-    ("T", 4, 0, 2, 4),
-    ("add", 4, 3),
-    ("F", 2),
-    ("B2", 1, 1),
-    ("Qf", 2),
-    ("S", 0, 1, 0, 7),
-    ("lo", 2),
     ("lb", 7),
-    ("mm", 5, 1),
-    ("A2", 1, 0),
+    ("lb", 8),
+    ("lb", 9),
+    ("lb", 10),
+    ("lr", 2),
+    ("lb", 11),
+    ("lo", 2),
+    ("beta",),
+    ("A2", 0, 0),
+    ("B1", 0),
+    ("mm", 0, 0, 0),
+    ("mm", 1, 0, 1),
+    ("add", 0, 0),
+    ("P2", 0, 0),
+    ("mm", 2, 0, 2),
+    ("add", 1, 0),
+    ("mm", 0, 1, 3),
+    ("add", 2, 0),
+    ("mm", 1, 1, 0),
+    ("add", 0, 1),
+    ("mm", 2, 1, 1),
+    ("add", 1, 1),
+    ("mm", 0, 2, 2),
+    ("F", 0),
+    ("B2", 0, 1),
+    ("mm", 1, 2, 3),
+    ("add", 2, 1),
+    ("T", 0, 0, 2, 4),
+    ("B1", 1),
+    ("T", 1, 0, 2, 5),
+    ("add", 0, 2),
+    ("mm", 2, 2, 0),
+    ("add", 1, 2),
+    ("C", 0, 0, 2),
+    ("mm", 0, 3, 1),
+    ("add", 2, 2),
+    ("C", 1, 0, 2),
+    ("mm", 1, 3, 2),
+    ("add", 0, 3),
+    ("mm", 2, 3, 3),
+    ("A2", 0, 2),
+    ("Qf", 0),
+    ("T", 2, 0, 2, 4),
+    ("T", 0, 2, 4, 5),
+    ("P2", 0, 2),
+    ("add", 1, 3),
+    ("C", 2, 0, 2),
+    ("mm", 3, 0, 0),
+    ("add", 2, 3),
+    ("C", 0, 2, 4),
+    ("mm", 4, 0, 1),
+    ("add", 3, 0),
+    ("T", 1, 2, 4, 4),
+    ("B2", 0, 3),
+    ("T", 2, 2, 4, 5),
+    ("C", 1, 2, 4),
+    ("mm", 5, 0, 2),
+    ("Q", 0),
+    ("C", 2, 2, 4),
+    ("mm", 3, 1, 3),
+    ("B1", 2),
+    ("add", 4, 0),
+    ("F", 1),
     ("S", 0, 0, 0, 6),
     ("add", 5, 0),
-    ("S", 0, 0, 1, 6),
-    ("mm", 5, 2),
-    ("mm", 5, 3),
+    ("mm", 4, 1, 0),
+    ("mm", 5, 1, 1),
+    ("add", 3, 1),
+    ("S", 0, 1, 0, 7),
+    ("add", 4, 1),
+    ("T", 3, 0, 2, 4),
     ("add", 5, 1),
-    ("C", 3, 2, 4),
-    ("S", 0, 0, 2, 6),
-    ("S", 0, 1, 1, 7),
-    ("T", 4, 2, 4, 5),
-    ("C", 4, 0, 2),
-    ("T", 5, 0, 2, 4),
-    ("Y", 0, 0),
-    ("add", 5, 2),
-    ("lb", 8),
-    ("S", 0, 1, 2, 7),
-    ("add", 5, 3),
+    ("T", 4, 0, 2, 5),
+    ("C", 3, 0, 2),
+    ("Q", 1),
+    ("mm", 3, 2, 2),
+    ("A2", 1, 0),
+    ("Qf", 1),
+    ("mm", 4, 2, 3),
+    ("mm", 5, 2, 0),
+    ("Q", 2),
+    ("F", 2),
+    ("add", 3, 2),
     ("P2", 1, 0),
-    ("Y", 0, 1),
-    ("S", 0, 2, 0, 6),
-    ("mm", 6, 0),
-    ("mm", 6, 1),
-    ("add", 6, 0),
-    ("B1", 3),
-    ("S", 0, 2, 1, 6),
-    ("mm", 6, 2),
-    ("S", 0, 3, 0, 7),
-    ("C", 4, 2, 4),
-    ("add", 6, 1),
+    ("T", 5, 0, 2, 4),
+    ("mm", 3, 3, 1),
+    ("add", 4, 2),
+    ("mm", 4, 3, 2),
+    ("add", 5, 2),
+    ("mm", 5, 3, 3),
+    ("B2", 1, 1),
+    ("C", 4, 0, 2),
+    ("S", 0, 0, 1, 6),
+    ("Qf", 2),
     ("C", 5, 0, 2),
+    ("S", 0, 1, 1, 7),
+    ("mm", 6, 0, 0),
+    ("add", 3, 3),
+    ("B1", 3),
     ("A2", 1, 2),
-    ("add", 6, 2),
-    ("Q", 3),
-    ("B2", 1, 3),
-    ("Q", 4),
-    ("P2", 1, 2),
-    ("mm", 6, 3),
-    ("mm", 7, 0),
-    ("S", 0, 2, 2, 6),
-    ("T", 5, 2, 4, 5),
-    ("T", 6, 0, 2, 4),
-    ("S", 0, 3, 1, 7),
-    ("mm", 7, 1),
-    ("st", 0, 0, 2),
-    ("B1", 4),
-    ("Y", 0, 2),
-    ("S", 0, 3, 2, 7),
-    ("C", 5, 2, 4),
-    ("mm", 7, 2),
-    ("add", 6, 3),
-    ("add", 7, 0),
-    ("add", 7, 1),
-    ("Y", 0, 3),
-    ("mm", 7, 3),
-    ("C", 6, 0, 2),
-    ("T", 6, 2, 4, 5),
-    ("add", 7, 2),
+    ("S", 0, 0, 2, 6),
+    ("add", 4, 3),
+    ("S", 0, 1, 2, 7),
+    ("T", 3, 2, 4, 5),
+    ("Y", 0, 0),
+    ("T", 4, 2, 4, 4),
+    ("Y", 0, 1),
+    ("C", 3, 2, 4),
+    ("mm", 6, 1, 1),
+    ("add", 5, 3),
     ("A2", 2, 0),
-    ("C", 6, 2, 4),
-    ("add", 7, 3),
-    ("P2", 2, 0),
-    ("T", 7, 0, 2, 4),
-    ("mm", 8, 0),
+    ("st", 0, 0, 2),
+    ("mm", 6, 2, 2),
+    ("P2", 1, 2),
+    ("add", 6, 0),
+    ("S", 0, 2, 0, 6),
+    ("C", 4, 2, 4),
+    ("S", 0, 3, 0, 7),
+    ("add", 6, 1),
+    ("S", 0, 2, 1, 6),
+    ("T", 5, 2, 4, 5),
+    ("Q", 3),
+    ("T", 6, 0, 2, 4),
+    ("Q", 4),
+    ("C", 5, 2, 4),
+    ("S", 0, 3, 1, 7),
+    ("S", 0, 2, 2, 6),
+    ("B2", 1, 3),
+    ("C", 6, 0, 2),
+    ("mm", 6, 3, 3),
     ("Q", 5),
+    ("mm", 7, 0, 0),
+    ("add", 6, 2),
+    ("B1", 4),
+    ("S", 0, 3, 2, 7),
+    ("mm", 7, 1, 1),
+    ("add", 6, 3),
+    ("mm", 7, 2, 2),
+    ("Y", 0, 2),
+    ("mm", 7, 3, 3),
+    ("add", 7, 0),
     ("S", 1, 0, 0, 6),
-    ("mm", 8, 1),
-    ("I", 0, 0),
-    ("B2", 2, 1),
-    ("B1", 5),
-    ("S", 1, 1, 0, 7),
+    ("add", 7, 1),
     ("S", 1, 0, 1, 6),
-    ("C", 7, 0, 2),
+    ("P2", 2, 0),
     ("S", 1, 0, 2, 6),
-    ("Q", 6),
-    ("Y", 1, 0),
-    ("mm", 8, 2),
-    ("S", 1, 1, 1, 7),
-    ("S", 1, 1, 2, 7),
-    ("mm", 8, 3),
-    ("add", 8, 0),
-    ("add", 8, 1),
+    ("Y", 0, 3),
+    ("T", 6, 2, 4, 5),
+    ("T", 7, 0, 2, 4),
+    ("add", 7, 2),
     ("st", 0, 2, 4),
-    ("Y", 1, 1),
+    ("C", 6, 2, 4),
+    ("mm", 8, 0, 0),
+    ("Y", 1, 0),
+    ("C", 7, 0, 2),
+    ("mm", 8, 1, 1),
+    ("B2", 2, 1),
     ("S", 1, 2, 0, 6),
-    ("S", 1, 2, 1, 6),
-    ("S", 1, 2, 2, 6),
-    ("T", 7, 2, 4, 5),
-    ("add", 8, 2),
-    ("T", 8, 0, 2, 4),
-    ("S", 1, 3, 0, 7),
-    ("S", 1, 3, 1, 7),
-    ("S", 1, 3, 2, 7),
-    ("S", 2, 1, 0, 1),
-    ("add", 8, 3),
-    ("S", 2, 0, 0, 0),
-    ("Y", 1, 2),
+    ("Q", 6),
+    ("S", 1, 1, 0, 7),
     ("A2", 2, 2),
-    ("C", 7, 2, 4),
-    ("T", 8, 2, 3, 5),
-    ("Q", 7),
-    ("T", 8, 3, 4, 6),
-    ("C", 8, 0, 2),
-    ("Y", 1, 3),
-    ("st", 1, 0, 2),
-    ("Qy", 0),
-    ("C", 8, 2, 3),
-    ("C", 8, 3, 4),
-    ("Q", 8, 0, 2),
-    ("S", 2, 3, 0, 3),
-    ("S", 2, 2, 0, 2),
-    ("S", 2, 3, 1, 3),
-    ("S", 2, 0, 1, 0),
-    ("S", 2, 2, 1, 2),
+    ("S", 1, 1, 1, 7),
+    ("B1", 5),
+    ("add", 7, 3),
+    ("mm", 8, 2, 2),
+    ("I", 0, 0),
+    ("add", 8, 0),
+    ("S", 1, 2, 1, 6),
+    ("S", 1, 1, 2, 7),
+    ("add", 8, 1),
+    ("mm", 8, 3, 3),
+    ("add", 8, 2),
+    ("T", 7, 2, 4, 5),
+    ("T", 8, 0, 2, 4),
+    ("Y", 1, 1),
     ("P2", 2, 2),
-    ("S", 2, 1, 1, 1),
-    ("Q", 8, 2, 4),
+    ("S", 1, 2, 2, 6),
+    ("add", 8, 3),
+    ("S", 2, 1, 0, 1),
+    ("C", 7, 2, 4),
+    ("st", 1, 0, 2),
+    ("S", 2, 2, 0, 2),
+    ("Y", 1, 2),
+    ("S", 1, 3, 0, 7),
+    ("C", 8, 0, 2),
+    ("S", 1, 3, 1, 7),
+    ("Q", 7),
+    ("S", 1, 3, 2, 7),
+    ("T", 8, 2, 3, 5),
+    ("T", 8, 3, 4, 6),
+    ("Y", 1, 3),
+    ("S", 2, 3, 0, 3),
+    ("C", 8, 2, 3),
+    ("S", 2, 2, 1, 2),
+    ("Qy", 0),
+    ("C", 8, 3, 4),
     ("st", 1, 2, 4),
-    ("S", 2, 0, 2, 0),
+    ("S", 2, 1, 1, 1),
     ("I", 1, 0),
+    ("S", 2, 0, 0, 0),
+    ("Q", 8, 0, 2),
+    ("S", 2, 3, 1, 3),
+    ("ss", 0),
+    ("Q", 8, 2, 4),
+    ("S", 2, 0, 1, 0),
+    ("sc", 0),
     ("B2", 2, 3),
+    ("S", 2, 0, 2, 0),
     ("S", 2, 1, 2, 1),
     ("S", 2, 2, 2, 2),
-    ("S", 2, 3, 2, 3),
     ("Y", 2, 0, 0),
-    ("sc", 0),
+    ("S", 2, 3, 2, 3),
     ("Y", 2, 1, 0),
     ("Y", 2, 2, 0),
+    ("st", 2, 0, 2, 0),
     ("Y", 2, 3, 0),
     ("Y", 2, 0, 1),
-    ("st", 2, 0, 4, 0),
+    ("st", 2, 2, 4, 0),
+    ("I", 2, 0, 0),
     ("Y", 2, 1, 1),
     ("Y", 2, 2, 1),
+    ("st", 2, 0, 2, 1),
     ("Y", 2, 3, 1),
-    ("st", 2, 0, 4, 1),
     ("Qy", 1),
-    ("I", 2, 0, 0),
+    ("st", 2, 2, 4, 1),
     ("I", 2, 1, 1),
     ("sc", 1),
     ("Qy", 2, 0),
-    ("sc", 2, 0),
     ("Qy", 2, 1),
+    ("sc", 2, 0),
+    ("ss", 1),
     ("sc", 2, 1),
-    ("ss",),
 ]
 
 
@@ -303,15 +311,18 @@ def tile_wpe_search_direction_k5_kernel(
             return keep.tile(shape, dtype, name=name, align_bytes=64)
 
         v_first = kept("v_first", [P, NT, 2 * P], U8)
-        v_sb = [kept("v_sb%d" % g, [P, NT, 2 * G], U8) for g in range(NG)]
+        v_head = kept("v_head", [P, NT, 2 * (G - P)], U8)
+        v_rest = kept("v_rest", [P, NT, 2 * (D - G)], U8)
         warm_in = kept("warm_in", [P, 4 * P], BF16)
         warm_codes = kept("warm_codes", [P, P], U32)
         warm_scales = kept("warm_scales", [P, P], U8)
-        x_sb = [kept("x_sb%d" % g, [P, NT, 2 * G], U8) for g in range(NG)]
+        x_first = kept("x_first", [P, NT, 2 * G], U8)
+        x_rest = kept("x_rest", [P, NT, 2 * (D - G)], U8)
         v_sc_first = kept("v_sc_first", [P, NT, G], U8)
         v_sc_rest = kept("v_sc_rest", [P, NT, D - G], U8)
-        x_sc = kept("x_sc", [P, NT, D], U8)
-        load_sb = [kept("load_sb%d" % b, [P, 4, G], BF16) for b in range(NB)]
+        x_sc_first = kept("x_sc_first", [P, NT, XF], U8)
+        x_sc_rest = kept("x_sc_rest", [P, NT, max(D - XF, 64)], U8)
+        load_sb = [kept("load_sb%d" % n, [P, D], BF16) for n in range(4 * NG)]
         filt_sb = [kept("filt_sb%d" % g, [P, 4, C], BF16) for g in range(NG)]
         rhs_sb = [kept("rhs_sb%d" % g, [P, 4, C], BF16) for g in range(NG)]
         old_sb = [kept("old_sb%d" % g, [P, 4, C], BF16) for g in range(NG)]
@@ -322,7 +333,8 @@ def tile_wpe_search_direction_k5_kernel(
         f_codes = [kept("f_codes%d" % g, [P, C], U32) for g in range(NG)]
         f_scales = [kept("f_scales%d" % g, [P, C], U8) for g in range(NG)]
         y_codes = [kept("y_codes%d" % g, [P, C], U32) for g in range(NG)]
-        y_scales = kept("y_scales", [P, NG, C], U8)
+        y_sc_early = kept("y_sc_early", [P, 1, C], U8)
+        y_sc_last = kept("y_sc_last", [P, NG - 1, C], U8)
         ident = kept("ident", [P, P], F32)
         step_bf = kept("step_bf", [P, NG, 4], BF16)
         step_pos = kept("step_pos", [P, NG * 4], F32)
@@ -338,20 +350,17 @@ def tile_wpe_search_direction_k5_kernel(
             view = src.bitcast(I32).rearrange("k p w -> p k w")
             nc.sync.dma_start(out=dst.bitcast(I32), in_=view[:, :, c0 // 2:c1 // 2])
 
-        def load_scales(queue, dst, src, c0, c1, quadrants):
-            view = src.bitcast(I32)
-            for q in quadrants:
-                rows = view[:, 4 * q:4 * q + 4, c0 // 4:c1 // 4].rearrange("k r w -> r k w")
-                queue.dma_start(out=dst[32 * q:32 * q + 4, :, :].bitcast(I32), in_=rows)
+        def load_scales(dst, src, c0, c1, rs):
+            view = src.bitcast(I32).rearrange("k (q r) w -> r q k w", r=4)
+            for r in rs:
+                nc.sync.dma_start(out=dst[r:P:32, :, :].bitcast(I32), in_=view[r][:, :, c0 // 4:c1 // 4])
 
-        def load_rows(dst, src, g):
-            nc.sync.dma_start(out=dst[g][:], in_=src[g * G:(g + 1) * G, :].rearrange("(p t) c -> p t c", t=4))
+        def load_rows(dst, src, g, t0=0, t1=4):
+            rows = src[g * G:(g + 1) * G, :].rearrange("(p t) c -> p t c", t=4)
+            nc.sync.dma_start(out=dst[g][:, t0:t1, :], in_=rows[:, t0:t1, :])
 
-        def load_block(b, u0=0, u1=4):
-            g, h = divmod(b, NG)
-            rows = loading[g * G:(g + 1) * G, h * G:(h + 1) * G].rearrange("(u p) j -> p u j", p=P)
-            nc.sync.dma_start(out=load_sb[b][:, u0:u1, :], in_=rows[:, u0:u1, :])
-
+        def load_block(n, c0=0, c1=D):
+            nc.sync.dma_start(out=load_sb[n][:, c0:c1], in_=loading[n * P:(n + 1) * P, c0:c1])
 
         corr = {}
         r_rows = {}
@@ -362,29 +371,32 @@ def tile_wpe_search_direction_k5_kernel(
         acc = {}
         scaled_old = {}
 
-        def correlate(b, u):
+        def correlate(b, u, n):
             g, h = divmod(b, NG)
-            out = bank(u, [P, G])
+            out = bank(n, [P, G])
             corr[b, u] = out
             v_sc, c0 = (v_sc_first, 0) if g == 0 else (v_sc_rest, (g - 1) * G)
+            col = g * G + u * P
+            v_tile, v0 = (v_first, 0) if col == 0 else (v_head, col - P) if g == 0 else (v_rest, col - G)
             for k in range(NT):
                 nc.tensor.matmul_mx(
                     out=out[:],
-                    lhsT=(v_first[:, k, :] if (g, u) == (0, 0) else v_sb[g][:, k, 256 * u:256 * (u + 1)]).bitcast(FP4X4),
+                    lhsT=v_tile[:, k, 2 * v0:2 * (v0 + P)].bitcast(FP4X4),
                     lhsT_scale=v_sc[:, k, c0 + P * u:c0 + P * (u + 1)],
-                    rhs=x_sb[h][:, k, :].bitcast(FP4X4),
-                    rhs_scale=x_sc[:, k, h * G:(h + 1) * G],
+                    rhs=(x_first[:, k, :] if h == 0 else x_rest[:, k, 2 * (h - 1) * G:2 * h * G]).bitcast(FP4X4),
+                    rhs_scale=x_sc_first[:, k, h * G:(h + 1) * G] if h * G < XF else x_sc_rest[:, k, h * G - XF:(h + 1) * G - XF],
                     start=(k == 0),
                     stop=(k == NT - 1),
                 )
 
         def add_loading(b, u):
+            g, h = divmod(b, NG)
             r = stage.tile([P, G], BF16, name="r_rows", tag="r_rows", bufs=8, align_bytes=64)
             r_rows[b, u] = r
             nc.vector.tensor_tensor(
                 out=r[:].rearrange("p (a w e) -> p a w e", a=2, e=2),
                 in0=corr[b, u][:].rearrange("p (w a e) -> p a w e", a=2, e=2),
-                in1=load_sb[b][:, u, :].rearrange("p (w a e) -> p a w e", a=2, e=2),
+                in1=load_sb[4 * g + u][:, h * G:(h + 1) * G].rearrange("p (w a e) -> p a w e", a=2, e=2),
                 op=ALU.add,
             )
 
@@ -398,7 +410,7 @@ def tile_wpe_search_direction_k5_kernel(
 
         def copy_turned(b, u0, u1):
             if u0 == 0:
-                r_turned[b] = stage.tile([P, 4 * G], BF16, name="r_turned", tag="r_turned", bufs=3, align_bytes=64)
+                r_turned[b] = stage.tile([P, 4 * G], BF16, name="r_turned", tag="r_turned", bufs=6, align_bytes=64)
             dst = r_turned[b][:].bitcast(F32).rearrange("p (t x a) -> p t x a", t=4, a=2)
             nc.scalar.copy(
                 out=dst[:, :, 32 * u0:32 * u1, :], in_=turned[b, u0][:].rearrange("p a (x t) -> p t x a", t=4)
@@ -483,7 +495,9 @@ def tile_wpe_search_direction_k5_kernel(
         def quantize_y(g, s=0):
             c0, c1 = columns(g, s)
             nc.vector.quantize_mx(
-                out=y_codes[g][:, c0:c1].bitcast(FP8X4), scales=y_scales[:, g, c0:c1], in_=y_il[g][:, 4 * c0:4 * c1]
+                out=y_codes[g][:, c0:c1].bitcast(FP8X4),
+                scales=y_sc_last[:, g - 1, c0:c1] if g else y_sc_early[:, 0, c0:c1],
+                in_=y_il[g][:, 4 * c0:4 * c1],
             )
 
         def store_codes(g, s=0):
@@ -503,22 +517,16 @@ def tile_wpe_search_direction_k5_kernel(
                 nc.tensor.transpose(bb[:, q, :], beta_col[:, q:q + 1].to_broadcast([P, P]), ident[:])
             nc.scalar.copy(out=beta_all[:].rearrange("p (c q) -> p c q", q=4), in_=bb[:].rearrange("p q c -> p c q"))
 
-        def store_scales():
-            scale_rows = out_2.bitcast(I32)
-            for q in range(4):
-                queue = nc.sync if q < 2 else nc.scalar
-                queue.dma_start(
-                    out=scale_rows[:, 4 * q:4 * q + 4, :].rearrange("g r w -> r g w"),
-                    in_=y_scales[32 * q:32 * q + 4, :, :].bitcast(I32),
-                )
+        def store_scales(last):
+            src, g0, g1 = (y_sc_last, 1, NG) if last else (y_sc_early, 0, 1)
+            scale_rows = out_2[g0:g1].bitcast(I32).rearrange("g (q r) w -> r q g w", r=4)
+            for r in range(4):
+                queue = nc.scalar if last and r >= 2 else nc.sync
+                queue.dma_start(out=scale_rows[r], in_=src[r:P:32, :, :].bitcast(I32))
 
         def load_small():
-            nc.sync.dma_start(out=beta_bf[:], in_=beta.rearrange("(p q) -> p q", q=4))
-            nc.sync.dma_start(out=step_bf[:], in_=step.rearrange("(g p t) -> p g t", p=P, t=4))
-
-        def load_v(g):
-            skip = P if g == 0 else 0
-            load_words(v_sb[g][:, :, 2 * skip:], v_words, g * G + skip, (g + 1) * G)
+            nc.scalar.dma_start(out=beta_bf[:], in_=beta.rearrange("(p q) -> p q", q=4))
+            nc.scalar.dma_start(out=step_bf[:], in_=step.rearrange("(g p t) -> p g t", p=P, t=4))
 
         def warm_up(passes):
             nc.vector.memset(warm_in[:], 1.0)
@@ -547,22 +555,23 @@ def tile_wpe_search_direction_k5_kernel(
             )
 
         actions = {
-            "ms": lambda n: nc.vector.memset((v_sc_first, x_sc, v_sc_rest)[n][:].bitcast(I32), 0),
+            "ms": lambda n: nc.vector.memset((v_sc_first, x_sc_first, v_sc_rest, x_sc_rest)[n][:].bitcast(I32), 0),
             "id": lambda: make_identity(nc, ident[:]),
             "warm": warm_up,
             "A2": scale_rhs,
             "P2": add_old,
             "lvf": lambda: load_words(v_first[:], v_words, 0, P),
-            "lsv": lambda q: load_scales(nc.sync, v_sc_first, v_scales, 0, G, (q,)),
-            "lsx": lambda q: load_scales(nc.sync, x_sc, x_scales, 0, D, (q,)),
+            "lsv": lambda q: load_scales(v_sc_first, v_scales, 0, G, (q,)),
+            "lsx": lambda q: load_scales(x_sc_first, x_scales, 0, XF, (q,)),
+            "lxs": lambda: load_scales(x_sc_rest, x_scales, XF, D, range(4)),
             "lsmall": load_small,
-            "lx": lambda h: load_words(x_sb[h][:], x_words, h * G, (h + 1) * G),
-            "lv": load_v,
-            "lvs": lambda: load_scales(nc.sync, v_sc_rest, v_scales, G, D, range(4)),
+            "lx": lambda n: load_words(x_rest[:], x_words, G, D) if n else load_words(x_first[:], x_words, 0, G),
+            "lv": lambda n: load_words(v_rest[:], v_words, G, D) if n else load_words(v_head[:], v_words, P, G),
+            "lvs": lambda: load_scales(v_sc_rest, v_scales, G, D, range(4)),
             "lb": load_block,
             "lf": lambda h: load_rows(filt_sb, filt, h),
-            "lo": lambda g: load_rows(old_sb, p_old, g),
-            "lr": lambda g: load_rows(rhs_sb, rhs, g),
+            "lo": lambda *a: load_rows(old_sb, p_old, *a),
+            "lr": lambda *a: load_rows(rhs_sb, rhs, *a),
             "mm": correlate,
             "add": add_loading,
             "T": turn,

from contextlib import ExitStack

import concourse.mybir as mybir
from concourse.masks import make_identity

F32 = mybir.dt.float32
BF16 = mybir.dt.bfloat16
I32 = mybir.dt.int32
U32 = mybir.dt.uint32
U8 = mybir.dt.uint8
FP4X4 = mybir.dt.float4_e2m1fn_x4
FP8X4 = mybir.dt.float8_e4m3fn_x4
ALU = mybir.AluOpType
ACT = mybir.ActivationFunctionType

T, D, C = 1024, 1536, 512
FLOPS = 2 * T * D * D + 2 * D * D * C

P = 128
G = 512
NG = D // G
NT = T // G
NB = NG * NG
XF = 512

ORDER = [
    ("id",),
    ("ms", 0),
    ("ms", 1),
    ("ms", 3),
    ("ms", 2),
    ("lr", 0, 0, 2),
    ("lsmall",),
    ("lb", 0, 0, 512),
    ("lvf",),
    ("lsv", 3),
    ("lsx", 2),
    ("lx", 1),
    ("lsv", 0),
    ("lsx", 0),
    ("lsv", 2),
    ("lsx", 3),
    ("lsx", 1),
    ("lo", 0, 0, 2),
    ("lx", 0),
    ("lsv", 1),
    ("lxs",),
    ("lv", 0),
    ("lb", 0, 512, 1536),
    ("lb", 1),
    ("lf", 0),
    ("lo", 0, 2, 4),
    ("lb", 2),
    ("lvs",),
    ("lb", 3),
    ("lr", 0, 2, 4),
    ("lv", 1),
    ("lb", 4),
    ("lo", 1),
    ("lf", 1),
    ("lb", 5),
    ("lr", 1),
    ("lf", 2),
    ("lb", 6),
    ("lb", 7),
    ("lb", 8),
    ("lb", 9),
    ("lb", 10),
    ("lr", 2),
    ("lb", 11),
    ("lo", 2),
    ("beta",),
    ("A2", 0, 0),
    ("B1", 0),
    ("mm", 0, 0, 0),
    ("mm", 1, 0, 1),
    ("add", 0, 0),
    ("P2", 0, 0),
    ("mm", 2, 0, 2),
    ("add", 1, 0),
    ("mm", 0, 1, 3),
    ("add", 2, 0),
    ("mm", 1, 1, 0),
    ("add", 0, 1),
    ("mm", 2, 1, 1),
    ("add", 1, 1),
    ("mm", 0, 2, 2),
    ("F", 0),
    ("B2", 0, 1),
    ("mm", 1, 2, 3),
    ("add", 2, 1),
    ("T", 0, 0, 2, 4),
    ("B1", 1),
    ("T", 1, 0, 2, 5),
    ("add", 0, 2),
    ("mm", 2, 2, 0),
    ("add", 1, 2),
    ("C", 0, 0, 2),
    ("mm", 0, 3, 1),
    ("add", 2, 2),
    ("C", 1, 0, 2),
    ("mm", 1, 3, 2),
    ("add", 0, 3),
    ("mm", 2, 3, 3),
    ("A2", 0, 2),
    ("Qf", 0),
    ("T", 2, 0, 2, 4),
    ("T", 0, 2, 4, 5),
    ("P2", 0, 2),
    ("add", 1, 3),
    ("C", 2, 0, 2),
    ("mm", 3, 0, 0),
    ("add", 2, 3),
    ("C", 0, 2, 4),
    ("mm", 4, 0, 1),
    ("add", 3, 0),
    ("T", 1, 2, 4, 4),
    ("B2", 0, 3),
    ("T", 2, 2, 4, 5),
    ("C", 1, 2, 4),
    ("mm", 5, 0, 2),
    ("Q", 0),
    ("C", 2, 2, 4),
    ("mm", 3, 1, 3),
    ("B1", 2),
    ("add", 4, 0),
    ("F", 1),
    ("S", 0, 0, 0, 6),
    ("add", 5, 0),
    ("mm", 4, 1, 0),
    ("mm", 5, 1, 1),
    ("add", 3, 1),
    ("S", 0, 1, 0, 7),
    ("add", 4, 1),
    ("T", 3, 0, 2, 4),
    ("add", 5, 1),
    ("T", 4, 0, 2, 5),
    ("C", 3, 0, 2),
    ("Q", 1),
    ("mm", 3, 2, 2),
    ("A2", 1, 0),
    ("Qf", 1),
    ("mm", 4, 2, 3),
    ("mm", 5, 2, 0),
    ("Q", 2),
    ("F", 2),
    ("add", 3, 2),
    ("P2", 1, 0),
    ("T", 5, 0, 2, 4),
    ("mm", 3, 3, 1),
    ("add", 4, 2),
    ("mm", 4, 3, 2),
    ("add", 5, 2),
    ("mm", 5, 3, 3),
    ("B2", 1, 1),
    ("C", 4, 0, 2),
    ("S", 0, 0, 1, 6),
    ("Qf", 2),
    ("C", 5, 0, 2),
    ("S", 0, 1, 1, 7),
    ("mm", 6, 0, 0),
    ("add", 3, 3),
    ("B1", 3),
    ("A2", 1, 2),
    ("S", 0, 0, 2, 6),
    ("add", 4, 3),
    ("S", 0, 1, 2, 7),
    ("T", 3, 2, 4, 5),
    ("Y", 0, 0),
    ("T", 4, 2, 4, 4),
    ("Y", 0, 1),
    ("C", 3, 2, 4),
    ("mm", 6, 1, 1),
    ("add", 5, 3),
    ("A2", 2, 0),
    ("st", 0, 0, 2),
    ("mm", 6, 2, 2),
    ("P2", 1, 2),
    ("add", 6, 0),
    ("S", 0, 2, 0, 6),
    ("C", 4, 2, 4),
    ("S", 0, 3, 0, 7),
    ("add", 6, 1),
    ("S", 0, 2, 1, 6),
    ("T", 5, 2, 4, 5),
    ("Q", 3),
    ("T", 6, 0, 2, 4),
    ("Q", 4),
    ("C", 5, 2, 4),
    ("S", 0, 3, 1, 7),
    ("S", 0, 2, 2, 6),
    ("B2", 1, 3),
    ("C", 6, 0, 2),
    ("mm", 6, 3, 3),
    ("Q", 5),
    ("mm", 7, 0, 0),
    ("add", 6, 2),
    ("B1", 4),
    ("S", 0, 3, 2, 7),
    ("mm", 7, 1, 1),
    ("add", 6, 3),
    ("mm", 7, 2, 2),
    ("Y", 0, 2),
    ("mm", 7, 3, 3),
    ("add", 7, 0),
    ("S", 1, 0, 0, 6),
    ("add", 7, 1),
    ("S", 1, 0, 1, 6),
    ("P2", 2, 0),
    ("S", 1, 0, 2, 6),
    ("Y", 0, 3),
    ("T", 6, 2, 4, 5),
    ("T", 7, 0, 2, 4),
    ("add", 7, 2),
    ("st", 0, 2, 4),
    ("C", 6, 2, 4),
    ("mm", 8, 0, 0),
    ("Y", 1, 0),
    ("C", 7, 0, 2),
    ("mm", 8, 1, 1),
    ("B2", 2, 1),
    ("S", 1, 2, 0, 6),
    ("Q", 6),
    ("S", 1, 1, 0, 7),
    ("A2", 2, 2),
    ("S", 1, 1, 1, 7),
    ("B1", 5),
    ("add", 7, 3),
    ("mm", 8, 2, 2),
    ("I", 0, 0),
    ("add", 8, 0),
    ("S", 1, 2, 1, 6),
    ("S", 1, 1, 2, 7),
    ("add", 8, 1),
    ("mm", 8, 3, 3),
    ("add", 8, 2),
    ("T", 7, 2, 4, 5),
    ("T", 8, 0, 2, 4),
    ("Y", 1, 1),
    ("P2", 2, 2),
    ("S", 1, 2, 2, 6),
    ("add", 8, 3),
    ("S", 2, 1, 0, 1),
    ("C", 7, 2, 4),
    ("st", 1, 0, 2),
    ("S", 2, 2, 0, 2),
    ("Y", 1, 2),
    ("S", 1, 3, 0, 7),
    ("C", 8, 0, 2),
    ("S", 1, 3, 1, 7),
    ("Q", 7),
    ("S", 1, 3, 2, 7),
    ("T", 8, 2, 3, 5),
    ("T", 8, 3, 4, 6),
    ("Y", 1, 3),
    ("S", 2, 3, 0, 3),
    ("C", 8, 2, 3),
    ("S", 2, 2, 1, 2),
    ("Qy", 0),
    ("C", 8, 3, 4),
    ("st", 1, 2, 4),
    ("S", 2, 1, 1, 1),
    ("I", 1, 0),
    ("S", 2, 0, 0, 0),
    ("Q", 8, 0, 2),
    ("S", 2, 3, 1, 3),
    ("ss", 0),
    ("Q", 8, 2, 4),
    ("S", 2, 0, 1, 0),
    ("sc", 0),
    ("B2", 2, 3),
    ("S", 2, 0, 2, 0),
    ("S", 2, 1, 2, 1),
    ("S", 2, 2, 2, 2),
    ("Y", 2, 0, 0),
    ("S", 2, 3, 2, 3),
    ("Y", 2, 1, 0),
    ("Y", 2, 2, 0),
    ("st", 2, 0, 2, 0),
    ("Y", 2, 3, 0),
    ("Y", 2, 0, 1),
    ("st", 2, 2, 4, 0),
    ("I", 2, 0, 0),
    ("Y", 2, 1, 1),
    ("Y", 2, 2, 1),
    ("st", 2, 0, 2, 1),
    ("Y", 2, 3, 1),
    ("Qy", 1),
    ("st", 2, 2, 4, 1),
    ("I", 2, 1, 1),
    ("sc", 1),
    ("Qy", 2, 0),
    ("Qy", 2, 1),
    ("sc", 2, 0),
    ("ss", 1),
    ("sc", 2, 1),
]


def tile_wpe_search_direction_k5_kernel(
    tc, v_words, v_scales, x_words, x_scales, loading, filt, rhs, step, beta, p_old, out_0, out_1, out_2
):
    nc = tc.nc
    with ExitStack() as ctx:
        keep = ctx.enter_context(tc.tile_pool(name="keep", bufs=1))
        stage = ctx.enter_context(tc.tile_pool(name="stage", bufs=1))
        psum = ctx.enter_context(tc.psum_pool(name="psum", bufs=1))
        ctx.enter_context(tc.manual_schedule())

        def kept(name, shape, dtype):
            return keep.tile(shape, dtype, name=name, align_bytes=64)

        v_first = kept("v_first", [P, NT, 2 * P], U8)
        v_head = kept("v_head", [P, NT, 2 * (G - P)], U8)
        v_rest = kept("v_rest", [P, NT, 2 * (D - G)], U8)
        warm_in = kept("warm_in", [P, 4 * P], BF16)
        warm_codes = kept("warm_codes", [P, P], U32)
        warm_scales = kept("warm_scales", [P, P], U8)
        x_first = kept("x_first", [P, NT, 2 * G], U8)
        x_rest = kept("x_rest", [P, NT, 2 * (D - G)], U8)
        v_sc_first = kept("v_sc_first", [P, NT, G], U8)
        v_sc_rest = kept("v_sc_rest", [P, NT, D - G], U8)
        x_sc_first = kept("x_sc_first", [P, NT, XF], U8)
        x_sc_rest = kept("x_sc_rest", [P, NT, max(D - XF, 64)], U8)
        load_sb = [kept("load_sb%d" % n, [P, D], BF16) for n in range(4 * NG)]
        filt_sb = [kept("filt_sb%d" % g, [P, 4, C], BF16) for g in range(NG)]
        rhs_sb = [kept("rhs_sb%d" % g, [P, 4, C], BF16) for g in range(NG)]
        old_sb = [kept("old_sb%d" % g, [P, 4, C], BF16) for g in range(NG)]
        parts = [1, 1, 2]
        y_sb = [kept("y_sb%d" % g, [P, parts[g], 4, C // parts[g]], F32) for g in range(NG)]
        r_codes = [kept("r_codes%d" % b, [P, G], U32) for b in range(NB)]
        r_scales = [kept("r_scales%d" % b, [P, G], U8) for b in range(NB)]
        f_codes = [kept("f_codes%d" % g, [P, C], U32) for g in range(NG)]
        f_scales = [kept("f_scales%d" % g, [P, C], U8) for g in range(NG)]
        y_codes = [kept("y_codes%d" % g, [P, C], U32) for g in range(NG)]
        y_sc_early = kept("y_sc_early", [P, 1, C], U8)
        y_sc_last = kept("y_sc_last", [P, NG - 1, C], U8)
        ident = kept("ident", [P, P], F32)
        step_bf = kept("step_bf", [P, NG, 4], BF16)
        step_pos = kept("step_pos", [P, NG * 4], F32)
        step_neg = kept("step_neg", [P, NG * 4], F32)
        beta_bf = kept("beta_bf", [P, 4], BF16)
        beta_col = kept("beta_col", [P, 4], F32)
        beta_all = kept("beta_all", [P, C], BF16)

        def bank(n, shape):
            return psum.tile(shape, F32, name="bank%d" % n, tag="bank%d" % n)

        def load_words(dst, src, c0, c1):
            view = src.bitcast(I32).rearrange("k p w -> p k w")
            nc.sync.dma_start(out=dst.bitcast(I32), in_=view[:, :, c0 // 2:c1 // 2])

        def load_scales(dst, src, c0, c1, rs):
            view = src.bitcast(I32).rearrange("k (q r) w -> r q k w", r=4)
            for r in rs:
                nc.sync.dma_start(out=dst[r:P:32, :, :].bitcast(I32), in_=view[r][:, :, c0 // 4:c1 // 4])

        def load_rows(dst, src, g, t0=0, t1=4):
            rows = src[g * G:(g + 1) * G, :].rearrange("(p t) c -> p t c", t=4)
            nc.sync.dma_start(out=dst[g][:, t0:t1, :], in_=rows[:, t0:t1, :])

        def load_block(n, c0=0, c1=D):
            nc.sync.dma_start(out=load_sb[n][:, c0:c1], in_=loading[n * P:(n + 1) * P, c0:c1])

        corr = {}
        r_rows = {}
        r_turned = {}
        turned = {}
        f_il = {}
        y_il = {}
        acc = {}
        scaled_old = {}

        def correlate(b, u, n):
            g, h = divmod(b, NG)
            out = bank(n, [P, G])
            corr[b, u] = out
            v_sc, c0 = (v_sc_first, 0) if g == 0 else (v_sc_rest, (g - 1) * G)
            col = g * G + u * P
            v_tile, v0 = (v_first, 0) if col == 0 else (v_head, col - P) if g == 0 else (v_rest, col - G)
            for k in range(NT):
                nc.tensor.matmul_mx(
                    out=out[:],
                    lhsT=v_tile[:, k, 2 * v0:2 * (v0 + P)].bitcast(FP4X4),
                    lhsT_scale=v_sc[:, k, c0 + P * u:c0 + P * (u + 1)],
                    rhs=(x_first[:, k, :] if h == 0 else x_rest[:, k, 2 * (h - 1) * G:2 * h * G]).bitcast(FP4X4),
                    rhs_scale=x_sc_first[:, k, h * G:(h + 1) * G] if h * G < XF else x_sc_rest[:, k, h * G - XF:(h + 1) * G - XF],
                    start=(k == 0),
                    stop=(k == NT - 1),
                )

        def add_loading(b, u):
            g, h = divmod(b, NG)
            r = stage.tile([P, G], BF16, name="r_rows", tag="r_rows", bufs=8, align_bytes=64)
            r_rows[b, u] = r
            nc.vector.tensor_tensor(
                out=r[:].rearrange("p (a w e) -> p a w e", a=2, e=2),
                in0=corr[b, u][:].rearrange("p (w a e) -> p a w e", a=2, e=2),
                in1=load_sb[4 * g + u][:, h * G:(h + 1) * G].rearrange("p (w a e) -> p a w e", a=2, e=2),
                op=ALU.add,
            )

        def turn(b, u0, u1, n):
            tb = bank(n, [P, 2, (u1 - u0) * P])
            turned[b, u0] = tb
            for u in range(u0, u1):
                words = r_rows[b, u][:].bitcast(F32)
                for a in range(2):
                    nc.tensor.transpose(tb[:, a, (u - u0) * P:(u - u0 + 1) * P], words[:, a * P:(a + 1) * P], ident[:])

        def copy_turned(b, u0, u1):
            if u0 == 0:
                r_turned[b] = stage.tile([P, 4 * G], BF16, name="r_turned", tag="r_turned", bufs=6, align_bytes=64)
            dst = r_turned[b][:].bitcast(F32).rearrange("p (t x a) -> p t x a", t=4, a=2)
            nc.scalar.copy(
                out=dst[:, :, 32 * u0:32 * u1, :], in_=turned[b, u0][:].rearrange("p a (x t) -> p t x a", t=4)
            )

        def quantize_r(b, t0=0, t1=4):
            nc.vector.quantize_mx(
                out=r_codes[b][:, P * t0:P * t1].bitcast(FP8X4),
                scales=r_scales[b][:, P * t0:P * t1],
                in_=r_turned[b][:, G * t0:G * t1],
            )

        def interleave(engine_copy, dst, src):
            engine_copy(out=dst.rearrange("p (c i t) -> p c t i", i=4, t=4), in_=src.rearrange("p t (c i) -> p c t i", i=4))

        def interleave_filt(h):
            f = stage.tile([P, 4 * C], BF16, name="f_il", tag="f_il", bufs=2, align_bytes=64)
            f_il[h] = f
            interleave(nc.scalar.copy, f[:], filt_sb[h][:])

        def quantize_filt(h):
            nc.vector.quantize_mx(out=f_codes[h][:].bitcast(FP8X4), scales=f_scales[h][:], in_=f_il[h][:])

        def apply_filter(g, t, h, n):
            if h == 0:
                acc[g, t] = bank(n, [P, C])
            b = g * NG + h
            nc.tensor.matmul_mx(
                out=acc[g, t][:],
                lhsT=r_codes[b][:, P * t:P * (t + 1)].bitcast(FP8X4),
                lhsT_scale=r_scales[b][:, P * t:P * (t + 1)],
                rhs=f_codes[h][:].bitcast(FP8X4),
                rhs_scale=f_scales[h][:],
                start=(h == 0),
                stop=(h == NG - 1),
            )

        def apply_all(g, t, n):
            for h in range(NG):
                apply_filter(g, t, h, n)

        def scale_old(k):
            g, s = divmod(k, 2)
            so = stage.tile([P, 2, C], F32, name="scaled_old", tag="scaled_old", bufs=1, align_bytes=64)
            scaled_old[k] = so
            for tt in range(2):
                nc.gpsimd.tensor_tensor(out=so[:, tt, :], in0=old_sb[g][:, 2 * s + tt, :], in1=beta_all[:], op=ALU.mult)

        def make_base(g, t):
            nc.vector.scalar_tensor_tensor(
                out=y_sb[g][:, :, t, :],
                in0=rhs_sb[g][:, t, :].rearrange("p (s c) -> p s c", s=parts[g]),
                scalar=step_pos[:, 4 * g + t:4 * g + t + 1],
                in1=scaled_old[2 * g + t // 2][:, t % 2, :].rearrange("p (s c) -> p s c", s=parts[g]),
                op0=ALU.mult,
                op1=ALU.add,
            )

        def columns(g, s):
            width = C // parts[g]
            return s * width, (s + 1) * width

        def finish(g, t, s=0):
            c0, c1 = columns(g, s)
            nc.vector.scalar_tensor_tensor(
                out=y_sb[g][:, s, t, :], in0=acc[g, t][:, c0:c1], scalar=step_neg[:, 4 * g + t:4 * g + t + 1],
                in1=y_sb[g][:, s, t, :], op0=ALU.mult, op1=ALU.add,
            )

        def store_y(g, t0, t1, s=0):
            c0, c1 = columns(g, s)
            rows = out_0[g * G:(g + 1) * G, :].rearrange("(p t) c -> p t c", t=4)
            nc.sync.dma_start(out=rows[:, t0:t1, c0:c1], in_=y_sb[g][:, s, t0:t1, :])

        def interleave_y(g, on_vector, s=0):
            c0, c1 = columns(g, s)
            engine_copy = nc.vector.tensor_copy if on_vector else nc.scalar.copy
            if s == 0:
                y_il[g] = stage.tile([P, 4 * C], BF16, name="y_il", tag="y_il", bufs=2, align_bytes=64)
            interleave(engine_copy, y_il[g][:, 4 * c0:4 * c1], y_sb[g][:, s, :, :])

        def quantize_y(g, s=0):
            c0, c1 = columns(g, s)
            nc.vector.quantize_mx(
                out=y_codes[g][:, c0:c1].bitcast(FP8X4),
                scales=y_sc_last[:, g - 1, c0:c1] if g else y_sc_early[:, 0, c0:c1],
                in_=y_il[g][:, 4 * c0:4 * c1],
            )

        def store_codes(g, s=0):
            c0, c1 = columns(g, s)
            words = out_1[g].rearrange("p m t -> p (m t)").bitcast(I32)
            nc.sync.dma_start(out=words[:, c0:c1], in_=y_codes[g][:, c0:c1].bitcast(I32))

        def spread_beta():
            nc.scalar.copy(out=beta_col[:], in_=beta_bf[:])
            nc.scalar.copy(out=step_pos[:], in_=step_bf[:].rearrange("p g t -> p (g t)"))
            nc.gpsimd.tensor_scalar(
                out=step_neg[:], in0=step_bf[:].rearrange("p g t -> p (g t)"),
                scalar1=-1.0, scalar2=0.0, op0=ALU.mult, op1=ALU.add,
            )
            bb = bank(6, [P, 4, P])
            for q in range(4):
                nc.tensor.transpose(bb[:, q, :], beta_col[:, q:q + 1].to_broadcast([P, P]), ident[:])
            nc.scalar.copy(out=beta_all[:].rearrange("p (c q) -> p c q", q=4), in_=bb[:].rearrange("p q c -> p c q"))

        def store_scales(last):
            src, g0, g1 = (y_sc_last, 1, NG) if last else (y_sc_early, 0, 1)
            scale_rows = out_2[g0:g1].bitcast(I32).rearrange("g (q r) w -> r q g w", r=4)
            for r in range(4):
                queue = nc.scalar if last and r >= 2 else nc.sync
                queue.dma_start(out=scale_rows[r], in_=src[r:P:32, :, :].bitcast(I32))

        def load_small():
            nc.scalar.dma_start(out=beta_bf[:], in_=beta.rearrange("(p q) -> p q", q=4))
            nc.scalar.dma_start(out=step_bf[:], in_=step.rearrange("(g p t) -> p g t", p=P, t=4))

        def warm_up(passes):
            nc.vector.memset(warm_in[:], 1.0)
            nc.vector.quantize_mx(out=warm_codes[:].bitcast(FP8X4), scales=warm_scales[:], in_=warm_in[:])
            out = bank(7, [P, P])
            for n in range(passes):
                nc.tensor.matmul_mx(
                    out=out[:], lhsT=warm_codes[:].bitcast(FP8X4), lhsT_scale=warm_scales[:],
                    rhs=warm_codes[:].bitcast(FP8X4), rhs_scale=warm_scales[:], start=True, stop=True,
                )

        def scale_rhs(g, t):
            nc.scalar.activation(
                out=y_sb[g][:, :, t, :],
                in_=rhs_sb[g][:, t, :].rearrange("p (s c) -> p s c", s=parts[g]),
                func=ACT.Copy,
                scale=step_pos[:, 4 * g + t:4 * g + t + 1],
            )

        def add_old(g, t):
            nc.gpsimd.tensor_tensor(
                out=y_sb[g][:, :, t, :],
                in0=y_sb[g][:, :, t, :],
                in1=scaled_old[2 * g + t // 2][:, t % 2, :].rearrange("p (s c) -> p s c", s=parts[g]),
                op=ALU.add,
            )

        actions = {
            "ms": lambda n: nc.vector.memset((v_sc_first, x_sc_first, v_sc_rest, x_sc_rest)[n][:].bitcast(I32), 0),
            "id": lambda: make_identity(nc, ident[:]),
            "warm": warm_up,
            "A2": scale_rhs,
            "P2": add_old,
            "lvf": lambda: load_words(v_first[:], v_words, 0, P),
            "lsv": lambda q: load_scales(v_sc_first, v_scales, 0, G, (q,)),
            "lsx": lambda q: load_scales(x_sc_first, x_scales, 0, XF, (q,)),
            "lxs": lambda: load_scales(x_sc_rest, x_scales, XF, D, range(4)),
            "lsmall": load_small,
            "lx": lambda n: load_words(x_rest[:], x_words, G, D) if n else load_words(x_first[:], x_words, 0, G),
            "lv": lambda n: load_words(v_rest[:], v_words, G, D) if n else load_words(v_head[:], v_words, P, G),
            "lvs": lambda: load_scales(v_sc_rest, v_scales, G, D, range(4)),
            "lb": load_block,
            "lf": lambda h: load_rows(filt_sb, filt, h),
            "lo": lambda *a: load_rows(old_sb, p_old, *a),
            "lr": lambda *a: load_rows(rhs_sb, rhs, *a),
            "mm": correlate,
            "add": add_loading,
            "T": turn,
            "C": copy_turned,
            "Q": quantize_r,
            "F": interleave_filt,
            "Qf": quantize_filt,
            "S": apply_filter,
            "beta": spread_beta,
            "B1": scale_old,
            "B2": make_base,
            "Y": finish,
            "st": store_y,
            "I": interleave_y,
            "Qy": quantize_y,
            "sc": store_codes,
            "ss": store_scales,
        }
        for token in ORDER:
            actions[token[0]](*token[1:])
